import numpy as np, ml_dtypes
CORES = [1,5,17,21,33,37,49,53]
N = 8
BF = ml_dtypes.bfloat16
L, S, NR, NC, RO, ST = 192, 16, 3072, 2048, 3, 3
def kill(rng, R, share):
    return np.where(rng.random((N, 8, 1, NR)) < share, 64, R)
def shares(rng):
    return np.stack([rng.permutation(np.array([0.1, 0.3, 0.3, 0.5, 0.5, 0.7, 0.7, 0.85])) for q in range(N)])[:, :, None, None]
def parts(rng):
    a = rng.choice(np.array([0.3, 1.0]), (N, 8, 1, NR))
    R = np.clip((16 + 32 * a * (rng.random((N, 8, 16, NR)) - 0.5)).astype(np.int64), 0, 31)
    H = rng.integers(90, 180, (N, 8, RO)) - 12 * np.arange(RO)
    return (rng.integers(0, 256, (N, 8, 16)), kill(rng, R, shares(rng)), rng.integers(0, NR, (N, 8, 16, NC)), rng.integers(0, 4096, (N, 8, NR)),
            rng.integers(0, 32, (N, 8, 16, L)), rng.integers(0, 4096, (N, 8, L)), np.maximum(H, 0))
def pack(w, R, C, P, Z, F, H):
    i = lambda a, *s: np.ascontiguousarray(a.reshape(*s)).astype(np.int32)
    return {"rec": np.ascontiguousarray(R.reshape(N, 128, NR)).astype(np.float32).astype(BF), "cel": i(C, N, 128, NC), "po": i(P, N, 8, NR),
            "pat": np.ascontiguousarray(Z.reshape(N, 128, L)).astype(np.float32).astype(BF), "phi": i(F, N, 8, L), "th": i(H, N, 8, RO), "wt": i(w, N, 128, 1)}
def lowest(ok, c):
    first = np.full((8, NC), L); lane = np.arange(L)[None, :]; g = np.arange(8)[:, None]
    np.minimum.at(first, (np.broadcast_to(g, c.shape), c), np.where(ok, lane, L))
    return ok & (first[g, c] == lane)
def look(R, C, Z, c):
    s = np.take_along_axis(C, c[:, None, :], 2)
    v = np.take_along_axis(R, s.reshape(8, 1, 16 * L), 2).reshape(8, 16, 16, L)
    return s, np.sum(np.abs(v - Z[:, :, None, :]), axis=1), v[:, 0] < 64
def at(a, k):
    return np.take_along_axis(a, k[:, None, :], 1)[:, 0]
def visit(R, C, P, Z, F, w, h, t):
    h1 = h[:, None, None]
    u = np.sum(w[:, :, None] * Z, axis=1) & 4095
    c = ((F * u >> 5) + F + 77 * t) & (NC - 1); e = ((c * u >> 5) + c + 1) & (NC - 1)
    s, d, live = look(R, C, Z, c); s2, d2, live2 = look(R, C, Z, e)
    sup = live & (d < h1); riv = live & (d >= h1)
    gain = 4 * np.sum(np.where(sup, h1 - d, 0), axis=1); loss = np.sum(np.where(riv, d - h1, 0), axis=1)
    acc = lowest(gain >= loss, c)
    has = np.any(sup, axis=1); y = np.argmin(np.where(sup, d, 9999), axis=1); ny = at(s, y)
    foe = np.any(riv, axis=1); nv = at(s, np.argmax(np.where(riv, d, -1), axis=1))
    zn = np.where(has[:, None, :], (Z + np.take_along_axis(R, ny[:, None, :], 2)) >> 1, Z)
    fn = np.where(acc & has, (np.take_along_axis(P, ny, 1) + 5 * at(d, y) + F) & 4095, (5 * F + u) & 4095)
    n = S * np.arange(L)[None, :] + (u & (S - 1))
    R2 = R.copy(); C2 = C.copy(); P2 = P.copy()
    g, i = np.nonzero(acc & foe); R2[g, :, nv[g, i]] = 64
    g, i = np.nonzero(acc); R2[g, :, n[g, i]] = zn[g, :, i]; P2[g, n[g, i]] = fn[g, i]
    g, i = np.nonzero(acc & np.any(~live, axis=1)); row = np.argmax(~live, axis=1)
    C2[g, row[g, i], c[g, i]] = n[g, i]
    acc2 = lowest(acc & ~np.any(live2 & (d2 < h1), axis=1), e)
    g, i = np.nonzero(acc2 & np.any(~live2, axis=1)); row = 15 - np.argmax(~live2[:, ::-1], axis=1)
    C2[g, row[g, i], e[g, i]] = n[g, i]
    return R2, C2, P2, zn, fn, acc
def setup_inputs(rng):
    return pack(*parts(rng))
def setup_inputs_spread(rng):
    w, R, C, P, Z, F, H = parts(rng)
    R = np.minimum((32 * rng.random((N, 8, 16, NR)) ** np.exp2(rng.integers(-2, 3, (N, 8, 1, NR)))).astype(np.int64), 31)
    Z = np.minimum((32 * rng.random((N, 8, 16, L)) ** np.exp2(rng.integers(-2, 3, (N, 8, 1, L)))).astype(np.int64), 31)
    C = np.minimum((NR * rng.random((N, 8, 16, NC)) ** 3).astype(np.int64), NR - 1)
    P = np.minimum(np.exp2(12 * rng.random((N, 8, NR))).astype(np.int64), 4095); F = np.minimum(np.exp2(12 * rng.random((N, 8, L))).astype(np.int64), 4095)
    w = np.minimum(np.exp2(8 * rng.random((N, 8, 16))).astype(np.int64), 255)
    H = np.where(rng.random((N, 8, RO)) < 0.6, rng.integers(60, 220, (N, 8, RO)), rng.integers(0, 481, (N, 8, RO)))
    return pack(w, kill(rng, R, shares(rng)), C, P, Z, F, H)
def edge(rng, n):
    k = rng.integers(0, 4, (N, 8, 1, n))
    return 31 * np.where(k <= 1, 0, np.where(k == 2, 1, rng.integers(0, 2, (N, 8, 16, n))))
def setup_inputs_ends(rng):
    w = 255 * rng.integers(0, 2, (N, 8, 16)); R = kill(rng, edge(rng, NR), 0.4); Z = edge(rng, L)
    C = np.where(rng.random((N, 8, 16, NC)) < 0.7, (NR - 1) * rng.integers(0, 2, (N, 8, 16, NC)), rng.integers(0, NR, (N, 8, 16, NC)))
    P = 4095 * rng.integers(0, 2, (N, 8, NR)); F = 4095 * rng.integers(0, 2, (N, 8, L)); H = 480 * rng.integers(0, 2, (N, 8, RO))
    for q in range(N):
        for g in range(6):
            R[q, g, :, 0] = (0, 31, 64)[(q + g) % 3]; R[q, g, :, NR - 1] = (0, 31, 64)[(q + g + 1) % 3]
    w[:, 5] = 0; w[:, 5, 0] = 195; Z[:, 5, 0, 0] = 21; F[:, 5, 0] = 4095
    R[:, 6] = 64; Z[:, 6] = 0; F[:, 6] = 0
    H[:, 7, 0] = 0; H[:, 7, 1] = 480; R[:, 7, :, 0] = 31; R[:, 7, :, NR - 1] = 0
    C[:, 7, :, 0] = 0; C[:, 7, :, NC - 1] = 0; C[:, 7, :, 77] = NR - 1
    for k in (0, 5, L - 2, L - 1):
        Z[:, 7, :, k] = 0; F[:, 7, k] = 0
    for q in range(N):
        a = visit(R[q], C[q], P[q], Z[q], F[q], w[q], H[q, :, 0], 0)[5]; a[6] = False
        m = 1 + ((30 - int(np.count_nonzero(a))) & 31)
        F[q, 6, rng.permutation(L)[:m - 1]] = np.arange(1, m)
    return pack(w, R, C, P, Z, F, H)
def selfsame(rng, u0, p0):
    p = np.arange(4096)[:, None]; u = np.arange(256)[None, :]
    c = ((p * u >> 5) + p) & (NC - 1); e = ((c * u >> 5) + c + 1) & (NC - 1)
    c0 = ((p0 * u0 >> 5) + p0) & (NC - 1); e0 = ((c0 * u0 >> 5) + c0 + 1) & (NC - 1)
    i, j = np.nonzero((c == e) & (c != c0) & (c != e0)); z = int(rng.integers(0, len(i)))
    return int(j[z]), int(i[z])
def setup_inputs_corners(rng):
    w, R, C, P, Z, F, H = parts(rng)
    for q in range(N):
        for g in range(8):
            o = (g + q) & 7
            if o == 0:
                R[q, g] = 64; Z[q, g] = 0; F[q, g] = rng.permutation(NC)[:L]
                w[q, g] = 0; w[q, g, 0] = 163; Z[q, g, 0, 0] = 25; F[q, g, 0] = 4093
                u, p = selfsame(rng, 4075, 4093)
                w[q, g, 1] = 1; w[q, g, 2] = 32; Z[q, g, 1, 1] = u & 31; Z[q, g, 2, 1] = u >> 5; F[q, g, 1] = p
            elif o == 1:
                R[q, g] = rng.integers(0, 32, (16, NR))
            elif o == 2:
                h = NR // 2; R[q, g, :, :h] = rng.integers(0, 32, (16, h)); R[q, g, :, h:] = 64
                C[q, g] = rng.integers(0, h, (16, NC)) + h * (np.arange(NC) & 1)[None, :]
                C[q, g, 15, 2::4] = h + rng.integers(0, h, NC // 4); C[q, g, 0, 3::4] = rng.integers(0, h, NC // 4)
            elif o == 3:
                C[q, g] = rng.integers(0, NR, (1, NC))
            elif o == 4:
                w[q, g] = 0; C[q, g] = S * rng.integers(0, L, (16, NC))
            elif o == 5:
                H[q, g] = 0; R[q, g] = np.where(R[q, g, :1] == 64, 64, 7 + (rng.random((1, NR)) < 0.1)); Z[q, g] = 7 + (rng.random((1, L)) < 0.1)
            elif o == 6:
                H[q, g] = 480; R[q, g] = np.where(R[q, g, :1] == 64, 64, 31 * rng.integers(0, 2, (1, NR))); Z[q, g] = 31 * rng.integers(0, 2, (1, L))
            else:
                w[q, g] = 255; C[q, g] = rng.choice(np.array([0, 1, S - 1, S, NR - S, NR - 2, NR - 1]), (16, NC))
                F[q, g] = 4095 * rng.integers(0, 2, L); P[q, g] = 4095 * rng.integers(0, 2, NR)
    return pack(w, R, C, P, Z, F, H)
def meet(rng):
    p = rng.integers(0, 4096, 1024)[:, None]; u = np.arange(1024)[None, :]
    c = ((p * u >> 5) + p) & (NC - 1); e = ((c * u >> 5) + c + 1) & (NC - 1); k = e[int(rng.integers(0, 1024)), int(rng.integers(512, 1024))]
    i, j = np.nonzero(e == k); o = rng.permutation(len(i)); i, j = i[o], j[o]
    x = np.resize(rng.permutation(np.unique(c[i, j], return_index=True)[1]), L); i, j = i[x], j[x]
    a, b = np.nonzero((e != k) & ~np.isin(c, c[i, j])); z = int(rng.integers(0, len(a)))
    return u[0, j], p[i, 0], int(u[0, b[z]]), int(p[a[z], 0])
def setup_inputs_crowd(rng):
    w, R, C, P, Z, F, H = parts(rng)
    for q in range(N):
        for g in range(8):
            o = (g + q) & 7; f0 = int(rng.integers(0, 4095))
            if q < 2:
                R[q, g] = 64; Z[q, g] = 0; F[q, g] = rng.permutation(NC)[:L]; H[q, g, 1] = int(rng.integers(220, 260))
            elif o <= 2:
                Z[q, g] = Z[q, g, :, :1].copy(); F[q, g] = f0; H[q, g, 0] = 480
                if o == 1: F[q, g, L - 1] = f0 + 1
                if o == 2: F[q, g, 1::2] = f0 + 1
            elif o <= 4:
                u, p, u1, p1 = meet(rng)
                if o == 4: u[L - 1] = u1; p[L - 1] = p1
                w[q, g] = 0; w[q, g, 0] = 1; w[q, g, 1] = 32; R[q, g] = 64; Z[q, g, 0] = u & 31; Z[q, g, 1] = u >> 5; F[q, g] = p
            elif o <= 6:
                w[q, g] = 0; R[q, g] = rng.integers(0, 4, (16, NR)); R[q, g, :, NR - 1] = 31; Z[q, g] = rng.integers(0, 4, (16, L)); F[q, g] = rng.permutation(NC)[:L]; H[q, g, 0] = 200
                C[q, g] = rng.integers(0, NR - 1, (16, NC)); C[q, g, rng.integers(0, 16, NC), np.arange(NC)] = NR - 1
                if o == 6: C[q, g, :, F[q, g, 3]] = rng.integers(0, NR - 1, 16)
            else:
                w[q, g] = 0; F[q, g] = f0; H[q, g, 0] = 150
    F[1, 7, L - 1] = F[1, 7, 0]
    return pack(w, R, C, P, Z, F, H)
def setup_inputs_ties(rng):
    w, R, C, P, Z, F, H = parts(rng)
    R = kill(rng, 8 * rng.integers(0, 2, (N, 8, 16, NR)), shares(rng)); Z = 8 * rng.integers(0, 2, (N, 8, 16, L)); H = 8 * rng.integers(4, 11, (N, 8, RO))
    C[:, :, 15] = np.where(rng.random((N, 8, NC)) < 0.3, C[:, :, 0], C[:, :, 15])
    return pack(w, R, C, P, Z, F, H)
def check_inputs(d):
    bad = []
    for k, lo, hi in (("rec", 0, 64), ("cel", 0, NR - 1), ("po", 0, 4095), ("pat", 0, 31), ("phi", 0, 4095), ("th", 0, 480), ("wt", 0, 255)):
        a = np.asarray(d[k]).astype(np.float64)
        if not (np.min(a) >= lo and np.max(a) <= hi and np.all(a == np.floor(a))): bad.append("range of " + k)
    a = np.asarray(d["rec"]).astype(np.float32).reshape(N, 8, 16, NR)
    if not np.all(np.all(a == 64, axis=2) | np.all(a <= 31, axis=2)): bad.append("a record of rec is neither living nor dead")
    return bad
def reference(rec, cel, po, pat, phi, th, wt):
    R = list(rec.astype(np.float32).astype(np.int32).reshape(N, 8, 16, NR)); C = list(cel.astype(np.int32).reshape(N, 8, 16, NC)); P = list(po.astype(np.int64))
    Z = list(pat.astype(np.float32).astype(np.int32).reshape(N, 8, 16, L)); F = list(phi.astype(np.int64))
    w = wt.astype(np.int32).reshape(N, 8, 16); H = th.astype(np.int64); A = [0] * N
    for t in range(RO):
        for q in range(N):
            R[q], C[q], P[q], Z[q], F[q], acc = visit(R[q], C[q], P[q], Z[q], F[q], w[q], H[q, :, t] + (A[q] & 31), t)
            A[q] = int(np.count_nonzero(acc))
        Z = [Z[(q - ST) % N] for q in range(N)]; F = [F[(q - ST) % N] for q in range(N)]
    return {"yrec": np.stack(R).reshape(N, 128, NR).astype(np.float32).astype(BF), "ycel": np.stack(C).reshape(N, 128, NC).astype(np.float32), "ypo": np.stack(P).astype(np.float32),
            "ypat": np.stack(Z).reshape(N, 128, L).astype(np.float32).astype(BF), "yphi": np.stack(F).astype(np.float32)}

@@ -1,0 +1,705 @@
+from concourse.mybir import AluOpType, AxisListType, ActivationFunctionType
+
+OP = AluOpType
+AF = ActivationFunctionType
+L, NR, NC, VIS, STEP = 192, 3072, 2048, 3, 3
+RW, CW = NR + L, NC + L
+POOLS = {"F": 15700, "I": 2900, "U": 1600, "B": 30800, "H": 10200}
+DTN = {"F": "float32", "I": "int32", "U": "uint16", "B": "bfloat16", "H": "float16"}
+SCRATCH = {
+    "rec_t": ("sbuf", [128, RW], "bfloat16"), "cel_t": ("sbuf", [128, CW], "float32"), "po_t": ("sbuf", [128, RW], "float32"),
+    "cel_i": ("sbuf", [128, NC], "int32"), "pod": ("dram", [8, NR], "float32"),
+    "zrep": ("sbuf", [128, 16 * L], "bfloat16"),
+}
+for _k in POOLS:
+    SCRATCH["pool" + _k] = ("sbuf", [128, POOLS[_k]], DTN[_k])
+for _t in range(1, VIS + 1):
+    SCRATCH["zl%d" % _t] = ("sbuf", [128, L], "bfloat16")
+    SCRATCH["pl%d" % _t] = ("sbuf", [128, 12 if _t < VIS else L], "float32")
+BANKS = ["b0", "b1", "b2", "b3", "b4", "b5", "e0", "e1"]
+for _b in BANKS:
+    SCRATCH[_b] = ("psum", [128, 512], "float32")
+SITE = {"dA": "b0", "kP": "b0", "hP": "b0", "tP": "b1", "zP": "b1", "vf": "b1", "ne": "b1", "de": "b2", "lP": "b2", "u": "b2", "s2": "b2",
+        "near": "b3", "dB": "b3", "acc": "b3", "xv": "b3", "fv": "b3", "nv": "b3", "s1": "b4", "nc": "b4", "xe": "b4", "fe": "b4", "aP": "b4",
+        "far": "b5", "xc": "b5", "fc": "b5", "win": "e0", "m1": "e0", "D1": "e0", "m2": "e1", "D2": "e1"}
+SEMAPHORES = ["sv", "sa", "sp", "sg", "ls"] + ["d%d" % i for i in range(20)] + ["rz%d" % t for t in (1, 2, 3)] + ["rp%d" % t for t in (1, 2, 3)]
+NS = 0.83 * 1.15e-3
+MAGIC = 12582912.0
+BIAS = {"acc0": 134, "far0": 42, "acc2": 102, "lists1": -68, "E22": 33, "zrep1": -111, "cg22": -1, "cell1": 234, "cell0": 81, "zrep2": -90,
+        "early1": 2, "ent10": -4, "phL1": 84, "cg02": 232, "n2": -140, "E11": -1, "cg10": 24, "cg11": 107, "ent21": 10, "cell2": -5, "ent22": -9,
+        "cg12": -1, "eg20": 1, "ent11": -43, "phL2": -34, "cg01": 54, "zrep0": 8, "E32": 338, "slots1": 37, "n1": -182, "n0": 115, "eg10": 1,
+        "lists2": -23, "ent12": -126, "far2": 163, "near2": 42, "E20": 3, "eg21": 2, "cg00": 62, "load": 59, "phL0": 2, "near1": -1, "ent20": 5,
+        "E10": 4, "ecell0": 17, "E12": 10, "near0": 181, "slots2": 53, "cg20": 64, "early2": 4, "ecell1": 3, "early0": 5, "cg21": 31, "E30": 80,
+        "newz2": -26, "eg22": -24, "newz1": 70, "eg12": 18, "far1": 97, "E21": -1, "eg02": 33, "eg11": -29, "eg00": -1, "ecell2": 1, "newz0": 9,
+        "E31": 25}
+CACHE = {}
+
+
+def build(ne):
+    ops, top, ndma, cur, vis = [], {k: 0 for k in POOLS}, [0], ["load"], []
+
+    def new(k, w):
+        o = top[k]
+        top[k] = o + (w + 15) // 16 * 16
+        if top[k] > POOLS[k]:
+            raise ValueError("pool %s is full" % k)
+        return ("pool" + k, o, w)
+
+    def r(t, c0=0, c1=None, st=1, p0=0, p1=128):
+        return ("R", t[0], t[1] + c0, t[1] + (t[2] if c1 is None else c1), st, p0, p1)
+
+    def ref(x):
+        return x if isinstance(x, (int, float)) or x is None or x[0] in ("R", "X") else r(x)
+
+    def ind(win, off):
+        return ("X", ref(win), ref(off))
+
+    ptop, sites = {b: 0 for b in BANKS}, {}
+
+    def place(site, w):
+        if site not in sites:
+            b = SITE[site]
+            sites[site] = (b, ptop[b], w)
+            ptop[b] += w
+            if ptop[b] > 512:
+                raise ValueError("bank %s is full" % b)
+        return sites[site]
+
+    def spans(x):
+        if x is None or isinstance(x, (int, float)):
+            return []
+        if x[0] == "X":
+            return spans(x[1]) + spans(x[2])
+        return [(x[1], x[2], x[3])]
+
+    def ncol(x):
+        return 16 * ncol(x[2]) if x[0] == "X" else (x[3] - x[2] + x[4] - 1) // x[4]
+
+    def ap(T, x):
+        if x is None or isinstance(x, (int, float)):
+            return x
+        if x[0] == "X":
+            return ap(T, x[1]).indirect(ap(T, x[2]))
+        t = T[x[1]]
+        return t[x[5]:x[6], x[2]:x[3]] if x[4] == 1 else t[x[5]:x[6], x[2]:x[3]:x[4]]
+
+    def two(x):
+        return x[0] == "R" and x[1] in ("poolB", "poolH", "poolU", "zrep", "rec_t")
+
+    def add(q, fn, reads, writes, cost, sem=None, val=1):
+        ops.append({"q": q, "fn": fn, "r": reads, "w": writes, "cost": cost, "sem": sem, "val": val, "i": len(ops),
+                    "tag": cur[0] + (str(vis[0]) if vis else "")})
+
+    def vcost(o, ins, rate):
+        n = ncol(o)
+        if o[0] == "X":
+            return 0.06 + n * 3.5 * NS
+        if any(x[0] == "X" for x in ins):
+            return 0.06 + n * 1.55 * NS
+        return 0.02 + max(64, n * rate) * NS
+
+    def vop(fn, outs, ins, cost):
+        add("v", fn, [s for x in ins for s in spans(x)], [s for x in outs for s in spans(x)], cost)
+
+    def vt(o, a, b, op):
+        o, a, b = ref(o), ref(a), ref(b)
+        both = a[0] == "R" and a[1] not in BANKS and b[1] not in BANKS
+        vop(lambda g, T: g.vector.tensor_tensor(out=ap(T, o), in0=ap(T, a), in1=ap(T, b), op=op), [o], [a, b], vcost(o, [a, b], 2 if both else 1))
+
+    def vs(o, a, s1, s2, op0, op1=None):
+        o, a, s1, s2 = ref(o), ref(a), ref(s1), ref(s2)
+        ex = {} if op1 is None else {"op1": op1}
+        vop(lambda g, T: g.vector.tensor_scalar(out=ap(T, o), in0=ap(T, a), scalar1=ap(T, s1), scalar2=ap(T, s2), op0=op0, **ex),
+            [o], [a, s1, s2], vcost(o, [a], 0.5 if two(o) and two(a) else 1))
+
+    def vc(o, a):
+        o, a = ref(o), ref(a)
+        vop(lambda g, T: g.vector.tensor_copy(out=ap(T, o), in_=ap(T, a)), [o], [a], vcost(o, [a], 0.5 if two(o) and two(a) else 1))
+
+    def vscan(o, d0, d1, init, o0, o1):
+        o, d0, d1 = ref(o), ref(d0), ref(d1)
+        vop(lambda g, T: g.vector.tensor_tensor_scan(out=ap(T, o), data0=ap(T, d0), data1=ap(T, d1), initial=init, op0=o0, op1=o1), [o], [d0, d1], vcost(o, [d0], 1))
+
+    def vtr(o, a):
+        o, a = ref(o), ref(a)
+        vop(lambda g, T: g.vector.transpose(out=ap(T, o), in_=ap(T, a)), [o], [a], vcost(o, [a], 1))
+
+    def vred(o, a):
+        o, a = ref(o), ref(a)
+        vop(lambda g, T: g.vector.tensor_reduce(out=ap(T, o), in_=ap(T, a), axis=AxisListType.X, op=OP.add), [o], [a], vcost(a, [a], 1))
+
+    def vm(o, c):
+        o = ref(o)
+        vop(lambda g, T: g.vector.memset(ap(T, o), c), [o], [], vcost(o, [o], 0.5 if two(o) else 1))
+
+    def act(o, a, f, scale=1.0, bias=0.0):
+        o, a, scale, bias = ref(o), ref(a), ref(scale), ref(bias)
+        x = a[0] == "X"
+        add("a", lambda g, T: g.scalar.activation(out=ap(T, o), in_=ap(T, a), func=f, bias=ap(T, bias), scale=ap(T, scale)),
+            [s for y in (a, scale, bias) for s in spans(y)], spans(o), (0.07 if x else 0.03) + max(64, ncol(o) * (1.55 if x else 1)) * NS)
+
+    def mm(ms):
+        ms = [(ref(o), ref(a), ref(b), s, e) for o, a, b, s, e in ms]
+
+        def fn(g, T):
+            k = None
+            for o, a, b, s, e in ms:
+                k = g.tensor.matmul(ap(T, o), ap(T, a), ap(T, b), s, e)
+            return k
+        rd = sorted(set(s for o, a, b, x, e in ms for y in (a, b) for s in spans(y)))
+        add("p", fn, rd, sorted(set(s for m in ms for s in spans(m[0]))), sum(max(64, ncol(m[2])) for m in ms) * NS + 0.03)
+
+    def iota(o, pat, base, cm):
+        o = ref(o)
+        add("g", lambda g, T: g.iota(ap(T, o), pat, base, cm), [], spans(o), 0.13 + 2 * ncol(o) * NS)
+
+    def dma(fn, reads, writes, cost, n=1):
+        add("s", fn, reads, writes, cost, "d%d" % ndma[0], 16 * n)
+        ndma[0] += 1
+
+    z, wI, thI, phI, poI = new("B", L), new("I", 1), new("I", 3), new("I", L), new("I", L)
+
+    def load(name, o, cost):
+        o = ref(o)
+        dma(lambda g, T: g.sync.dma_start(out=ap(T, o), in_=T[name][:]), [], spans(o), cost)
+    load("phi", r(phI, p1=8), 2.2)
+    load("pat", z, 2.2)
+    load("wt", wI, 2.2)
+    load("th", r(thI, p1=8), 2.2)
+    for h in (0, 1):
+        cs = ("cel_i", 1024 * h, 1024)
+        dma(lambda g, T, h=h: g.sync.dma_start(out=T.cel_i[:, 1024 * h:1024 * h + 1024], in_=T.cel[:, 1024 * h:1024 * h + 1024]), [], spans(ref(cs)), 4.0 + 2 * h)
+    dma(lambda g, T: g.sync.dma_start(out=T.rec_t[:, 0:NR], in_=T.rec[:]), [], [("rec_t", 0, NR)], 8.5)
+    load("po", poI, 9.0)
+
+    cur[0] = "const"
+    pI, yI, iI, xI, bI, wyp = new("I", 1), new("I", 128), new("I", L), new("I", 144), new("I", 12), new("I", 128)
+    i12, j6 = new("I", 96), new("I", 6)
+    iota(pI, [[0, 1]], 0, 1)
+    iota(iI, [[1, L]], 0, 0)
+    iota(xI, [[1, 144]], -15, 0)
+    iota(yI, [[1, 128]], 0, 0)
+    iota(wyp, [[1, 128]], 0, -1)
+    iota(bI, [[1, 12]], 0, 0)
+    iota(i12, [[0, 8], [1, 12]], 0, 0)
+    iota(j6, [[16, 6]], 0, 1)
+    kI, gI, hI = new("I", 1), new("I", 1), new("I", 1)
+    kc, gc, ec, oc, pg, pc = [new("F", 1) for i in range(6)]
+    vs(kI, pI, 15, None, OP.bitwise_and)
+    vs(gI, pI, 4, None, OP.arith_shift_right)
+    vs(hI, gI, 1, None, OP.bitwise_and)
+    vc(kc, kI); vc(gc, gI); vc(oc, hI); vc(pc, pI)
+    vs(ec, oc, -1.0, 1.0, OP.mult, OP.add)
+    vs(pg, gc, 16.0, None, OP.mult)
+    i15 = new("I", L)
+    diag, M0, RS = new("F", L), new("F", L), new("F", L)
+    vs(i15, iI, 15, None, OP.bitwise_and)
+    vs(diag, i15, kc, None, OP.is_equal)
+    vs(M0, i15, 0.0, None, OP.is_gt)
+    act(RS, M0, AF.Identity, 2.0e9, -1.0e9)
+    U, UW, wc = new("B", 144), new("B", 144), new("F", 1)
+    vs(U, xI, pg, None, OP.is_equal)
+    vc(wc, wI)
+    vs(UW, U, wc, None, OP.mult)
+    ygI, BO, sel8 = new("I", 128), new("H", 128), new("H", 128)
+    vs(ygI, yI, 4, None, OP.arith_shift_right)
+    vs(BO, ygI, gc, None, OP.is_equal)
+    vs(r(sel8, p1=8), r(ygI, p1=8), r(pc, p1=8), None, OP.is_equal)
+    ph16, th16, thc = new("H", L), new("H", 3), new("F", 3)
+    vs(r(ph16, p1=8), r(phI, p1=8), -2048.0, None, OP.add)
+    vs(r(th16, p1=8), r(thI, p1=8), 0.0, None, OP.add)
+    xq = place("xc", L)
+    mm([(xq, r(sel8, p1=8), r(ph16, p1=8), True, True)])
+    pm, ps, phi = new("F", L), new("F", L), new("F", 12)
+    vt(pm, xq, diag, OP.mult)
+    vscan(ps, M0, pm, 0.0, OP.mult, OP.add)
+    vs(phi, r(ps, 15, L, 16), 2048.0, None, OP.add)
+    tp = r(place("u", 12), 0, 3)
+    mm([(tp, r(sel8, p1=8), r(th16, p1=8), True, True)])
+    vc(thc, tp)
+    dumR, dumC, i16A, bl = new("F", 12), new("F", 12), new("F", 12), new("U", 12)
+    vs(i16A, bI, 16.0, kc, OP.mult, OP.add)
+    act(dumR, i16A, AF.Identity, 1.0, float(NR))
+    act(dumC, i16A, AF.Identity, 1.0, float(NC))
+    dumS, dumRC = new("F", 12), new("F", 24)
+    act(dumS, dumR, AF.Identity, 1.0, -1536.0)
+    act(r(dumRC, 0, 12), dumR, AF.Copy)
+    act(r(dumRC, 12, 24), dumC, AF.Copy)
+    act(i16A, i16A, AF.Identity, 16.0)
+    vc(bl, bI)
+    m3, m1, bo8 = new("B", 8), new("B", 8), new("B", 8)
+    vc(bo8, r(BO, 0, 128, 16))
+    act(m3, bo8, AF.Identity, -3.0)
+    act(m1, bo8, AF.Identity, -1.0)
+    one = new("B", 128)
+    vm(one, 1.0)
+    DW, MSK, list2 = new("B", 240), new("F", 96), new("U", 6)
+    vm(DW, 0.0)
+    vc(r(DW, 112, 128), r(diag, 0, 16))
+    mb1 = new("F", 96)
+    vs(mb1, i12, 8.0, 4.0, OP.is_ge, OP.mult)
+    vt(mb1, i12, mb1, OP.subtract)
+    vs(MSK, mb1, gc, None, OP.is_equal)
+    ja, jb, jf = new("I", 6), new("I", 6), new("F", 6)
+    vs(jf, j6, pg, None, OP.subtract)
+    vs(ja, jf, 1.0 / 12, 0.5 / 12 - 0.5, OP.mult, OP.add)
+    vs(jb, jf, 1.0 / 12, 4.5 / 12 - 0.5, OP.mult, OP.add)
+    vt(jf, ja, jb, OP.add)
+    vc(list2, jf)
+    pw, d16, scol, t1c, hf = new("F", 16), new("F", 16), new("F", 1), new("F", 1), new("F", 32)
+    vm(r(hf, 0, 16), 0.5); vm(r(hf, 16, 32), 0.0)
+    vscan(pw, r(hf, 0, 16), r(hf, 16, 32), 2.0, OP.mult, OP.add)
+    vt(d16, pw, r(diag, 0, 16), OP.mult)
+    vred(scol, d16)
+    klt, k10, k11, k12, k13 = [new("F", 1) for i in range(5)]
+    vs(klt, kc, 12.0, None, OP.is_lt)
+    for kk, v in ((k10, 10.0), (k11, 11.0), (k12, 12.0), (k13, 13.0)):
+        vs(kk, kc, v, None, OP.is_equal)
+    vt(scol, scol, klt, OP.mult)
+    vs(t1c, klt, -0.5, None, OP.mult)
+    fb, fs, gb, gs, fbe, fse, fbo, fso, t2c = [new("F", 1) for i in range(9)]
+    vs(t2c, k10, 2.0, t1c, OP.mult, OP.add)
+    vt(fb, t2c, k12, OP.add)
+    vt(gb, t2c, k13, OP.add)
+    vs(fs, k13, -1.0 / 512, klt, OP.mult, OP.add)
+    vs(gs, k12, 1.0 / 512, klt, OP.mult, OP.add)
+    vt(fbe, fb, ec, OP.mult); vt(fse, fs, ec, OP.mult); vt(fbo, fb, oc, OP.mult); vt(fso, fs, oc, OP.mult)
+    I16, L16, laneC, t128, kv = new("H", 128), new("H", 128), new("H", L), new("F", 128), new("F", 1)
+    vs(I16, wyp, 0.0, None, OP.is_equal)
+    vs(kv, kc, 0.0, None, OP.is_gt)
+    vt(kv, kv, klt, OP.mult)
+    vs(kv, kv, -2.0, None, OP.mult)
+    vs(t128, wyp, -1.0, kv, OP.is_equal, OP.mult)
+    vt(L16, t128, I16, OP.add)
+    vt(t1c, k12, k13, OP.add)
+    vs(laneC, iI, t1c, None, OP.mult)
+    TL, TH, tl = new("B", 128), new("B", 128), new("F", 128)
+    vs(tl, wyp, 0.0, None, OP.is_gt)
+    vt(tl, tl, BO, OP.mult)
+    vt(TL, I16, tl, OP.subtract)
+    vs(t128, wyp, 0.0, None, OP.is_lt)
+    vt(t128, t128, BO, OP.mult)
+    vt(TH, I16, t128, OP.subtract)
+    nI, hI16, kI16, q25 = new("B", 128), new("B", 128), new("B", 128), new("B", L)
+    vs(nI, wyp, 0.0, -1.0, OP.is_equal, OP.mult)
+    act(hI16, nI, AF.Identity, -0.5)
+    act(kI16, nI, AF.Identity, 1024.0)
+    act(q25, M0, AF.Identity, 0.0, -0.25)
+    C2, pw2, bM, hf2 = new("H", L), new("F", 16), new("F", 1), new("F", 16)
+    vm(hf2, 2.0)
+    vscan(pw2, hf2, r(hf, 16, 32), 0.5, OP.mult, OP.add)
+    vt(d16, pw2, r(diag, 0, 16), OP.mult)
+    vred(t2c, d16)
+    vs(t2c, t2c, -0.5, 0.5, OP.mult, OP.add)
+    vt(t2c, t2c, klt, OP.mult)
+    vs(C2, M0, 0.0, t2c, OP.mult, OP.add)
+    vs(bM, k11, MAGIC, None, OP.add)
+    pas, acc, cand, winB, vfB = [new("B", 16) for i in range(5)]
+    P = [[new("H", 128), new("H", 128)], [new("H", 128), new("H", 128)]]
+    vs(P[0][0], wyp, 0.0, ec, OP.is_equal, OP.mult)
+    vs(P[1][1], wyp, 0.0, oc, OP.is_equal, OP.mult)
+    vs(P[0][1], wyp, 16.0, ec, OP.is_equal, OP.mult)
+    vs(P[1][0], wyp, -16.0, oc, OP.is_equal, OP.mult)
+    knear = new("F", 1)
+    vs(knear, kc, -1.0 / 16, 255.0 + 15.0 / 16, OP.mult, OP.add)
+    c128, c64 = new("B", L), new("B", L)
+    act(c128, M0, AF.Identity, 0.0, 128.0)
+    act(c64, M0, AF.Identity, 0.0, 64.0)
+    vm(("rec_t", NR, L), 64.0)
+    vm(("po_t", NR, L), 0.0)
+    for h in (0, 1):
+        vc(("cel_t", 1024 * h, 1024), ("cel_i", 1024 * h, 1024))
+    poF = new("F", L)
+    vc(poF, poI)
+    dma(lambda g, T: g.sync.dma_start(out=T.pod[:], in_=ap(T, r(poF))), spans(r(poF)), [("pod", 0, 1)], 2.2)
+    fan_id = ndma[0]
+
+    def fan(g, T):
+        k = None
+        for i in range(16):
+            k = g.sync.dma_start(out=T.po_t[i::16, 0:NR], in_=T.pod[:])
+            if i < 15:
+                k.then_inc(T.sem["d%d" % fan_id], 16)
+        return k
+    dma(fan, [("pod", 0, 1)], [("po_t", 0, NR)], 7.0, 16)
+    h = new("F", 1)
+    vc(h, r(thc, 0, 1))
+    celw, celn, recw, recn, pow_ = ("cel_t", 0, CW), ("cel_t", 0, NC), ("rec_t", 0, RW), ("rec_t", 0, NR), ("po_t", 0, RW)
+    Es = [new("B", 2048) for x in range(3)]
+    dfad = [(new("B", 1024), new("B", 1024)) for x in range(6)]
+
+    def expand(src):
+        X = new("H", L)
+        vt(X, ind(src, bl), diag, OP.mult)
+        return X
+
+    def pairs(val, E, site):
+        X, Vi, Vh = expand(val), new("F", L), new("H", L)
+        xP, fp = place("x" + site, L), place("f" + site, L)
+        mm([(xP, BO, X, True, False), (xP, I16, C2, False, True)])
+        act(Vi, xP, AF.Identity, scol, bM)
+        vs(Vh, Vi, -MAGIC, None, OP.add)
+        mm([(fp, L16, Vh, True, False), (fp, I16, laneC, False, True)])
+        G, Fe, Fo = new("B", L), new("B", L), new("B", L)
+        act(Fe, fp, AF.Identity, fse, fbe)
+        act(G, fp, AF.Identity, gs, gb)
+        act(Fo, fp, AF.Identity, fso, fbo)
+        for a in range(4):
+            bank, ms = ("e1", "e0")[a & 1], []
+            for x, F in ((0, Fe), (1, Fo)):
+                pp = {"p0": 32 * a, "p1": 32 * a + 32}
+                ms.append(((bank, 256 * x, L), r(F, 0, 128, **pp), r(G, **pp), True, True))
+                ms.append(((bank, 256 * x + L, 64), r(F, 64, L, **pp), r(G, 128, L, **pp), True, True))
+            mm(ms)
+            act(r(E, 512 * a, 512 * a + 512), (bank, 0, 512), AF.Relu, 512.0, -1536.0)
+        return E
+
+    def lowest(vec, E, site, out):
+        q, ms = place("n" + site, 16), []
+        for g in range(8):
+            h0, h1 = r(vec, 2 * g, 2 * g + 1), r(vec, 2 * g + 1, 2 * g + 2, p0=64)
+            ms.append((r(q, 2 * g, 2 * g + 1), r(E, 256 * g, 256 * g + 128), h0, True, True))
+            ms.append((r(q, 2 * g + 1, 2 * g + 2), r(E, 256 * g + 64, 256 * g + L), h0, True, False))
+            ms.append((r(q, 2 * g + 1, 2 * g + 2), r(E, 256 * g + 128, 256 * g + 256, p0=64), h1, False, True))
+        mm(ms)
+        vt(out, vec, q, OP.is_gt)
+        return out
+
+    def score(terms, site, extra=None):
+        for q, a, b in ((r(place(site, 16), 0, 16, 2), 0, 128), (r(place(site, 16), 1, 16, 2), 64, L)):
+            ms = [(q, r(x, a, b), y) for x, y in terms]
+            if extra:
+                ms.append((q, extra[0], extra[1]))
+            mm([m + (i == 0, i == len(ms) - 1) for i, m in enumerate(ms)])
+
+    def to_a(vec, site):
+        X = new("B", 96)
+        vt(X, ind(vec, list2), MSK, OP.mult)
+        q = place(site, 12)
+        mm([(q, r(DW, 112 - 16 * g, 240 - 16 * g), r(X, 12 * g, 12 * g + 12), g == 0, g == 7) for g in range(8)])
+        return q
+
+    def best(key, site, parts):
+        kt, ks, q = new("F", L), new("F", L), place(site, 24)
+        ki, k2, kp = new("I", 12), new("I", 24), new("H", 24)
+        for a, b in parts:
+            vtr(r(kt, a, b), r(key, a, b))
+            vscan(r(ks, a, b), r(RS, a, b), r(kt, a, b), -1.0e9, OP.min, OP.max)
+        vs(ki, r(ks, 15, L, 16), 65536.0, None, OP.mult)
+        vs(r(k2, 0, 12), ki, 4095, None, OP.bitwise_and)
+        vs(r(k2, 12, 24), ki, 16, None, OP.arith_shift_right)
+        vs(kp, k2, -1536.0, None, OP.add)
+        mm([(r(q, ih, 24, 2), P[ih][x], r(kp, x, 24, 2), x == 0, x == 1) for ih in (0, 1) for x in (0, 1)])
+        return r(q, 0, 12), r(q, 12, 24)
+
+    def send(src, name, sem):
+        src = ref(src)
+
+        def fn(g, T, me, dst, topo):
+            rid, pid, se = topo.addr(dst)
+            return g.remote_dma(T[name][:], ap(T, src), T.sem[sem], T.sem.ls, pid, rid, topo.mask(me, dst))
+        add("g", fn, spans(src), [(name + "_sent", 0, 1)], 1.0, "ls", ne)
+        add("net", None, [(name + "_sent", 0, 1)], [(name, 0, SCRATCH[name][1][1])], 2.5, sem, ne)
+
+    for t in range(VIS):
+        last = t == VIS - 1
+        vis[:] = [t]
+        cur[0] = "cell"
+        h5, hm, h511, hmat, hdead = new("F", 1), new("F", 1), new("F", 1), new("H", 8), new("H", 8)
+        act(h5, h, AF.Identity, 5.0)
+        act(hm, h, AF.Identity, -1.0, 512.0)
+        act(h511, h, AF.Identity, 1.0, -511.0)
+        vs(hmat, bo8, h511, None, OP.mult)
+        vs(hdead, bo8, hm, None, OP.mult)
+        cur[0] = "zrep"
+        for k in range(16):
+            act(r(("zrep", 0, 16 * L), k, 16 * L, 16), z, AF.Copy)
+        cur[0] = "cell"
+        uP = place("u", 12)
+        mm([(uP, r(UW, 15 - k, 143 - k), r(z, k, L, 16), k == 0, k == 15) for k in range(16)])
+        uI, u, ma, mb, mc, c, c1, e = [new("I", 12) for i in range(8)]
+        c16, e16 = new("U", 12), new("U", 12)
+        vc(uI, uP)
+        vs(u, uI, 4095, None, OP.bitwise_and)
+        vt(ma, phi, u, OP.mult)
+        vs(mb, ma, 5, None, OP.arith_shift_right)
+        p77 = phi
+        if t:
+            p77 = new("F", 12)
+            act(p77, phi, AF.Identity, 1.0, 77.0 * t)
+        vt(mc, mb, p77, OP.add)
+        vs(c, mc, NC - 1, None, OP.bitwise_and)
+        vc(c16, c)
+        sc16, se16 = new("U", L), new("U", L)
+        vc(sc16, ind(celn, c16))
+        cur[0] = "ecell"
+        me, mf, mg = [new("I", 12) for i in range(3)]
+        vt(me, c, u, OP.mult)
+        vs(mf, me, 5, None, OP.arith_shift_right)
+        vs(c1, c, 1.0, None, OP.add)
+        vt(mg, mf, c1, OP.add)
+        vs(e, mg, NC - 1, None, OP.bitwise_and)
+        vc(e16, e)
+        vc(se16, ind(celn, e16))
+        dc = lambda a, b: r(place("dA", 128), a, b) if b <= 128 else r(place("dB", 64), a - 128, b - 128)
+        for s16, dst in ((sc16, dc), (se16, lambda a, b: r(place("de", L), a, b))):
+            for ch in range(3):
+                cur[0] = ("cg" if s16 is sc16 else "eg") + str(ch)
+                df, ad = dfad[ch + (0 if s16 is sc16 else 3)]
+                for x in (0, 1):
+                    w = 1024 * ch + 512 * x
+                    vt(r(df, 512 * x, 512 * x + 512), ind(recn, r(s16, 64 * ch + 32 * x, 64 * ch + 32 * x + 32)), ("zrep", w, 512), OP.subtract)
+                    act(r(ad, 512 * x, 512 * x + 512), r(df, 512 * x, 512 * x + 512), AF.Abs)
+                q = dst(64 * ch, 64 * ch + 64)
+                mm([(q, r(U, 15 - k, 143 - k), r(ad, k, 1024, 16), k == 0, k == 15) for k in range(16)])
+        cur[0] = "early"
+        n15, n, pa, pb, P2 = new("I", 12), new("F", 12), new("F", 12), new("I", 12), new("I", 12)
+        vs(n15, u, 15, None, OP.bitwise_and)
+        vt(n, n15, i16A, OP.add)
+        act(pa, phi, AF.Identity, 5.0)
+        vt(pb, pa, u, OP.add)
+        vs(P2, pb, 4095, None, OP.bitwise_and)
+        skN, sc32, s16c = new("F", L), new("F", L), new("H", L)
+        act(sc32, ind(celn, c16), AF.Copy)
+        act(skN, sc32, AF.Identity, 2.0 ** -16, knear)
+        vs(s16c, sc16, -1536.0, None, OP.add)
+        cm, em = new("F", 12), new("F", 12)
+        vs(cm, c, -1024.0, None, OP.add)
+        cur[0] = "E1"
+        E1 = pairs(cm, Es[0], "c")
+        cur[0] = "E2"
+        vs(em, e, -1024.0, None, OP.add)
+        E2 = pairs(em, Es[1], "e")
+        cur[0] = "n"
+        nm = new("F", 12)
+        act(nm, n, AF.Identity, 1.0, -1536.0)
+        Xn = expand(nm)
+        cur[0] = "slots"
+        q1, q2, K1, K2, dead = new("H", L), new("H", L), new("F", L), new("F", L), new("B", L)
+        for a, b in ((0, 128), (128, L)):
+            d = dc(a, b)
+            vt(r(K1, a, b), r(skN, a, b), d, OP.subtract)
+            vs(r(q1, a, b), d, 512.0, -511.0, OP.min, OP.add)
+            vs(r(q2, a, b), r(q1, a, b), h511, h511, OP.min, OP.subtract)
+            vs(r(dead, a, b), r(q1, a, b), 1.0, None, OP.is_ge)
+        cur[0] = "far"
+        kP = place("kP", L)
+        mm([(kP, I16, q1, True, False), (kP, kI16, dead, False, True)])
+        vt(K2, skN, kP, OP.add)
+        cur[0] = "near"
+        nyP, dd = best(K1, "near", ((0, 128), (128, L)))
+        ny16, d5, has = new("U", 12), new("F", 12), new("F", 12)
+        vs(ny16, nyP, 1536.0, None, OP.add)
+        act(d5, dd, AF.Identity, -5.0, 1275.0 - 5 * 1536.0)
+        vs(has, d5, h5, None, OP.is_lt)
+        pog, pos, pd, Pa, P1, Dp, Dh = new("F", L), new("F", L), new("F", 12), new("I", 12), new("I", 12), new("F", 12), new("F", 12)
+        vt(pog, ind(pow_, ny16), diag, OP.mult)
+        vscan(pos, M0, pog, 0.0, OP.mult, OP.add)
+        vt(pd, d5, phi, OP.add)
+        vt(Pa, r(pos, 15, L, 16), pd, OP.add)
+        vs(P1, Pa, 4095, None, OP.bitwise_and)
+        vt(Dp, P1, P2, OP.subtract)
+        vt(Dh, Dp, has, OP.mult)
+        cur[0] = "newz"
+        hP, tP, zP = place("hP", L), place("tP", L), place("zP", L)
+        hs, rz, zw, zm, zn = new("B", L), new("B", L), new("B", L), new("F", L), new("B", L)
+        mm([(hP, BO, q2, True, True)])
+        act(hs, hP, AF.Sign, -1.0)
+        act(rz, ind(recw, ny16), AF.Copy)
+        mm([(tP, I16, rz, True, False), (tP, nI, z, False, True)])
+        vt(zw, hs, tP, OP.mult)
+        mm([(zP, I16, z, True, False), (zP, hI16, zw, False, False), (zP, I16, q25, False, True)])
+        act(zm, zP, AF.Identity, 1.0, MAGIC)
+        act(zn, zm, AF.Identity, 1.0, -MAGIC)
+        send(zn, "zl%d" % (t + 1), "rz%d" % (t + 1))
+        cur[0] = "far"
+        vP, fd = best(K2, "far", ((0, L),))
+        vm_, riv, vd, vdr = new("F", 12), new("F", 12), new("F", 12), new("F", 12)
+        vs(riv, fd, 256.0 + 1536.0, h, OP.add, OP.is_ge)
+        vt(vd, vP, dumS, OP.subtract)
+        vt(vdr, vd, riv, OP.mult)
+        vt(vm_, vdr, dumS, OP.add)
+        cur[0] = "E3"
+        E3 = pairs(vm_, Es[2], "v")
+        cur[0] = "acc"
+        score([(q1, m1), (q2, m3), (dead, hdead)], "s1", (one, hmat))
+        vs(pas, place("s1", 16), 0.0, None, OP.is_ge)
+        lowest(pas, E1, "c", acc)
+        accA = to_a(acc, "acc")
+        ft, phN = new("F", 12), new("F", 12)
+        vt(ft, Dh, accA, OP.mult)
+        vt(phN, ft, P2, OP.add)
+        if not last:
+            send(phN, "pl%d" % (t + 1), "rp%d" % (t + 1))
+        cur[0] = "phL"
+        ph2, phL, lP = new("F", 12), new("F", L), place("lP", L)
+        act(ph2, phN, AF.Identity, 1.0, -2048.0)
+        X = expand(ph2)
+        mm([(lP, BO, X, True, False), (lP, BO, c128, False, True)])
+        act(phL, lP, AF.Identity)
+        if last:
+            send(phL, "pl%d" % VIS, "rp%d" % VIS)
+        else:
+            aP, aF, aI, aJ = place("aP", 16), new("F", 1), new("I", 1), new("I", 1)
+            mm([(r(aP, 0, 16, 2), one, r(acc, 0, 16, 2), True, True), (r(aP, 1, 16, 2), r(one, p0=64), r(acc, 1, 16, 2, p0=64), True, True)])
+            vred(aF, aP)
+            vc(aI, aF)
+            vs(aJ, aI, 31, None, OP.bitwise_and)
+        cur[0] = "E3"
+        vfA = to_a(lowest(acc, E3, "v", vfB), "vf")
+        tv, ov, v16 = new("F", 12), new("F", 12), new("U", 12)
+        vt(tv, vdr, vfA, OP.mult)
+        vt(ov, tv, dumR, OP.add)
+        vc(v16, ov)
+        cur[0] = "lists"
+        nd_, cd_, tn, on, u24 = new("F", 12), new("F", 12), new("F", 24), new("F", 24), new("U", 24)
+        vt(nd_, n, dumR, OP.subtract)
+        vt(cd_, c, dumC, OP.subtract)
+        vt(r(tn, 0, 12), nd_, accA, OP.mult)
+        vt(r(tn, 12, 24), cd_, accA, OP.mult)
+        vt(on, tn, dumRC, OP.add)
+        vc(u24, on)
+        n16, cw = r(u24, 0, 12), r(u24, 12, 24)
+        vc(ind(recw, v16), c64)
+        vc(ind(recw, n16), zn)
+        vc(ind(pow_, n16), phL)
+        cur[0] = "ent1"
+        M1, ch1, mP, DP = new("F", L), new("F", L), place("m1", L), place("D1", L)
+        mm([(mP, TL, dead, True, True), (DP, BO, Xn, True, False), (DP, nI, s16c, False, True)])
+        act(M1, mP, AF.Relu)
+        vt(ch1, M1, DP, OP.mult)
+        vt(ind(celw, cw), ch1, sc32, OP.add)
+        cur[0] = "ent2"
+        q1e, q2e, deade = new("H", L), new("H", L), new("B", L)
+        vs(q1e, place("de", L), 512.0, -511.0, OP.min, OP.add)
+        vs(q2e, q1e, h511, h511, OP.min, OP.subtract)
+        vs(deade, q1e, 1.0, None, OP.is_ge)
+        score([(q2e, m1)], "s2")
+        vt(cand, acc, place("s2", 16), OP.is_gt)
+        wA = to_a(lowest(cand, E2, "e", winB), "win")
+        ed, et, eo, ew = new("F", 12), new("F", 12), new("F", 12), new("U", 12)
+        vt(ed, e, dumC, OP.subtract)
+        vt(et, ed, wA, OP.mult)
+        vt(eo, et, dumC, OP.add)
+        vc(ew, eo)
+        M2, sE, s16e, ch2, mP, DP = new("F", L), new("F", L), new("H", L), new("F", L), place("m2", L), place("D2", L)
+        act(sE, ind(celn, e16), AF.Copy)
+        vs(s16e, sE, -1536.0, None, OP.add)
+        mm([(mP, TH, deade, True, True), (DP, BO, Xn, True, False), (DP, nI, s16e, False, True)])
+        act(M2, mP, AF.Relu)
+        vt(ch2, M2, DP, OP.mult)
+        vt(ind(celw, ew), ch2, sE, OP.add)
+        if not last:
+            h = new("F", 1)
+            vt(h, aJ, r(thc, t + 1, t + 2), OP.add)
+            z, phi = ("zl%d" % (t + 1), 0, L), ("pl%d" % (t + 1), 0, 12)
+    dma(lambda g, T: g.sync.dma_start(out=T.ypat[:], in_=T["zl%d" % VIS][:]), [("zl%d" % VIS, 0, L)], [("ypat", 0, 1)], 2.2)
+    dma(lambda g, T: g.sync.dma_start(out=T.yphi[:], in_=T["pl%d" % VIS][::16, :]), [("pl%d" % VIS, 0, L)], [("yphi", 0, 1)], 2.2)
+    dma(lambda g, T: g.sync.dma_start(out=T.ypo[:], in_=T.po_t[::16, 0:NR]), [("po_t", 0, NR)], [("ypo", 0, 1)], 3.0)
+    dma(lambda g, T: g.sync.dma_start(out=T.yrec[:], in_=T.rec_t[:, 0:NR]), [("rec_t", 0, NR)], [("yrec", 0, 1)], 5.0)
+    dma(lambda g, T: g.sync.dma_start(out=T.ycel[:], in_=T.cel_t[:, 0:NC]), [("cel_t", 0, NC)], [("ycel", 0, 1)], 6.0)
+    return ops
+
+
+def depend(ops):
+    hist, deps = {}, []
+    for o in ops:
+        d = set()
+        acc = [(s, False) for s in o["r"]] + [(s, True) for s in o["w"]]
+        for (buf, lo, hi), wr in acc:
+            ps = buf in BANKS
+            for (k, a, b, w) in hist.get(buf, []):
+                hit = (w or wr) and a < hi and lo < b
+                if (ops[k]["q"] != o["q"] or (o["q"] != "p" and hit)) if ps else hit:
+                    d.add(k)
+        for (buf, lo, hi), wr in acc:
+            hh = hist.setdefault(buf, [])
+            if wr and buf not in BANKS:
+                hist[buf] = hh = [x for x in hh if not (lo <= x[1] and x[2] <= hi)]
+            hh.append((o["i"], lo, hi, wr))
+        d.discard(o["i"])
+        deps.append(d)
+    return deps
+
+
+def schedule(ops, deps):
+    n = len(ops)
+    succ = [[] for i in range(n)]
+    for i, d in enumerate(deps):
+        for k in d:
+            succ[k].append(i)
+    lat = lambda k, i: 0.05 if ops[k]["q"] == ops[i]["q"] else (0.12 if ops[k]["q"] != "net" else 0.3)
+    pr = [0.0] * n
+    for i in range(n - 1, -1, -1):
+        pr[i] = ops[i]["cost"] + max([lat(i, j) + pr[j] for j in succ[i]] or [0.0])
+    left = [len(d) for d in deps]
+    ready = {i for i in range(n) if not left[i]}
+    rt, free, order, end = [0.0] * n, {}, [], [0.0] * n
+    while ready:
+        pick, cand = None, {}
+        for i in sorted(ready):
+            cand.setdefault(ops[i]["q"], []).append(i)
+        for q, li in cand.items():
+            f = free.get(q, 0.0) if q != "net" else 0.0
+            s0 = min(max(f, rt[i]) for i in li)
+            b = max((i for i in li if max(f, rt[i]) <= s0 + 0.04), key=lambda i: (pr[i] + BIAS.get(ops[i]["tag"], 0.0), -i))
+            s = max(f, rt[b])
+            if pick is None or s < pick[0]:
+                pick = (s, b, q)
+        s, i, q = pick
+        ready.discard(i)
+        free[q] = s + (0.1 if q == "s" else ops[i]["cost"])
+        end[i] = s + ops[i]["cost"]
+        order.append(i)
+        for j in succ[i]:
+            rt[j] = max(rt[j], end[i] + lat(i, j))
+            left[j] -= 1
+            if not left[j]:
+                ready.add(j)
+    return order, max(end)
+
+
+QSEM = {"v": "sv", "a": "sa", "p": "sp"}
+
+
+def plan(ne):
+    if "plan" not in CACHE:
+        ops = build(ne)
+        deps = depend(ops)
+        order, span = schedule(ops, deps)
+        CACHE["plan"] = (ops, deps, order, span)
+    return CACHE["plan"]
+
+
+def rank_program(g, core, T, topo):
+    rank = T.rank_of(core)
+    if rank is None:
+        return
+    me, dst = T.cores[rank], T.cores[(rank + STEP) % len(T.cores)]
+    ops, deps, order, span = plan(len(topo.engines(me, dst)))
+    eng = {"v": g.vector, "a": g.scalar, "p": g.tensor, "g": g, "s": g.sync}
+    at, count, seen = {}, {}, {}
+    for i in order:
+        o = ops[i]
+        q = o["q"]
+        sem = o["sem"] or QSEM.get(q, "sg")
+        count[sem] = count.get(sem, 0) + o["val"]
+        at[i] = (sem, count[sem])
+        if q == "net":
+            continue
+        need = {}
+        for k in deps[i]:
+            s, v = at[k]
+            if s == "ls" or (q == "p" and ops[k]["q"] == "p"):
+                continue
+            need[s] = max(need.get(s, 0), v)
+        for s in sorted(need):
+            if seen.get((q, s), 0) < need[s]:
+                eng[q].wait_ge(T.sem[s], need[s])
+                seen[(q, s)] = need[s]
+        if o["sem"] == "ls":
+            o["fn"](g, T, me, dst, topo)
+        else:
+            o["fn"](g, T).then_inc(T.sem[sem], 1 if o["sem"] is None else 16)
+    for s in sorted(count):
+        g.sync.wait_ge(T.sem[s], count[s])

@@ -4,7 +4,7 @@ OP = AluOpType
 AF = ActivationFunctionType
 L, NR, NC, VIS, STEP = 192, 3072, 2048, 3, 3
 RW, CW = NR + L, NC + L
-POOLS = {"F": 15700, "I": 2900, "U": 1600, "B": 30800, "H": 10200}
+POOLS = {"F": 19000, "I": 2900, "U": 1600, "B": 33000, "H": 10200}
 DTN = {"F": "float32", "I": "int32", "U": "uint16", "B": "bfloat16", "H": "float16"}
 SCRATCH = {
     "rec_t": ("sbuf", [128, RW], "bfloat16"), "cel_t": ("sbuf", [128, CW], "float32"), "po_t": ("sbuf", [128, RW], "float32"),
@@ -25,13 +25,13 @@ SITE = {"dA": "b0", "kP": "b0", "hP": "b0", "tP": "b1", "zP": "b1", "vf": "b1", 
 SEMAPHORES = ["sv", "sa", "sp", "sg", "ls"] + ["d%d" % i for i in range(20)] + ["rz%d" % t for t in (1, 2, 3)] + ["rp%d" % t for t in (1, 2, 3)]
 NS = 0.83 * 1.15e-3
 MAGIC = 12582912.0
-BIAS = {"acc0": 134, "far0": 42, "acc2": 102, "lists1": -68, "E22": 33, "zrep1": -111, "cg22": -1, "cell1": 234, "cell0": 81, "zrep2": -90,
-        "early1": 2, "ent10": -4, "phL1": 84, "cg02": 232, "n2": -140, "E11": -1, "cg10": 24, "cg11": 107, "ent21": 10, "cell2": -5, "ent22": -9,
-        "cg12": -1, "eg20": 1, "ent11": -43, "phL2": -34, "cg01": 54, "zrep0": 8, "E32": 338, "slots1": 37, "n1": -182, "n0": 115, "eg10": 1,
-        "lists2": -23, "ent12": -126, "far2": 163, "near2": 42, "E20": 3, "eg21": 2, "cg00": 62, "load": 59, "phL0": 2, "near1": -1, "ent20": 5,
-        "E10": 4, "ecell0": 17, "E12": 10, "near0": 181, "slots2": 53, "cg20": 64, "early2": 4, "ecell1": 3, "early0": 5, "cg21": 31, "E30": 80,
-        "newz2": -26, "eg22": -24, "newz1": 70, "eg12": 18, "far1": 97, "E21": -1, "eg02": 33, "eg11": -29, "eg00": -1, "ecell2": 1, "newz0": 9,
-        "E31": 25}
+BIAS = {"ent11": 205, "early1": -530, "far1": 307, "ent12": 315, "far2": 112, "newz0": 492, "cg11": 736, "phL2": 73, "acc2": 31, "ent10": -55,
+        "cg02": 227, "cg22": 638, "load": 630, "cg12": 434, "near2": -74, "eg12": 8, "ecell2": -5, "acc0": 73, "n0": -120, "ecell0": -376,
+        "E21": 125, "n1": -151, "cg01": 238, "n2": -497, "lists2": 251, "ecell1": 3, "E20": -2, "zrep2": -222, "E31": 317, "early2": -60,
+        "E30": 339, "cell2": 160, "cg10": 75, "eg01": 183, "eg02": 110, "newz2": -221, "eg21": 107, "ent20": 1, "phL0": -531, "slots0": 348,
+        "newz1": 132, "zrep0": 67, "acc1": 106, "eg22": 159, "eg11": 20, "far0": 892, "cg20": -1, "cg21": 220, "phL1": -162, "ent21": -1,
+        "slots2": 5, "near1": 242, "E32": -62, "E10": 112, "cg00": 605, "ent22": -73, "slots1": 218, "eg10": 5, "zrep1": -73, "cell0": 4,
+        "lists0": -9, "lists1": -3, "near0": 2, "cell1": -1}
 CACHE = {}
 
 
@@ -128,10 +128,6 @@ def build(ne):
         o, a = ref(o), ref(a)
         vop(lambda g, T: g.vector.tensor_reduce(out=ap(T, o), in_=ap(T, a), axis=AxisListType.X, op=OP.add), [o], [a], vcost(a, [a], 1))
 
-    def vm(o, c):
-        o = ref(o)
-        vop(lambda g, T: g.vector.memset(ap(T, o), c), [o], [], vcost(o, [o], 0.5 if two(o) else 1))
-
     def act(o, a, f, scale=1.0, bias=0.0):
         o, a, scale, bias = ref(o), ref(a), ref(scale), ref(bias)
         x = a[0] == "X"
@@ -151,7 +147,11 @@ def build(ne):
 
     def iota(o, pat, base, cm):
         o = ref(o)
-        add("g", lambda g, T: g.iota(ap(T, o), pat, base, cm), [], spans(o), 0.13 + 2 * ncol(o) * NS)
+        add("g", lambda g, T: g.iota(ap(T, o), pat, base, cm, allow_small_or_imprecise_dtypes=True), [], spans(o), 0.13 + 2 * ncol(o) * NS)
+
+    def sel(o, a, pat, base, cm, fill, cmp_):
+        o, a = ref(o), ref(a)
+        add("g", lambda g, T: g.affine_select(ap(T, o), ap(T, a), pat, cmp_, fill, base, cm), spans(a), spans(o), 0.17 + 2 * ncol(o) * NS)
 
     def dma(fn, reads, writes, cost, n=1):
         add("s", fn, reads, writes, cost, "d%d" % ndma[0], 16 * n)
@@ -173,39 +173,39 @@ def build(ne):
     load("po", poI, 9.0)
 
     cur[0] = "const"
-    pI, yI, iI, xI, bI, wyp = new("I", 1), new("I", 128), new("I", L), new("I", 144), new("I", 12), new("I", 128)
-    i12, j6 = new("I", 96), new("I", 6)
-    iota(pI, [[0, 1]], 0, 1)
-    iota(iI, [[1, L]], 0, 0)
-    iota(xI, [[1, 144]], -15, 0)
-    iota(yI, [[1, 128]], 0, 0)
-    iota(wyp, [[1, 128]], 0, -1)
-    iota(bI, [[1, 12]], 0, 0)
+
+    def col(a, scale=1.0, bias=0.0, f=AF.Identity, k="F"):
+        o = new(k, ref(a)[3] - ref(a)[2])
+        act(o, a, f, scale, bias)
+        return o
+
+    def same(a, neg, k="F"):
+        return col(col(a, 1.0, neg, AF.Abs), -1.0, 1.0, AF.Relu, k)
+
+    def tile(a, scale, bias=0.0):
+        return col(a, scale, bias, AF.Identity, "B")
+    p2, pF, yg, i15, b12, j6, xF, iF = new("F", 1), new("F", 1), new("F", 128), new("F", L), new("F", 12), new("F", 6), new("F", 144), new("F", L)
+    p4, i12 = new("F", 1), new("F", 96)
+    iota(p2, [[0, 1]], -15, 2)
+    iota(pF, [[0, 1]], 0, 1)
+    iota(yg, [[1, 8], [0, 16]], 0, 0)
+    iota(i15, [[0, 12], [1, 16]], 0, 0)
+    iota(xF, [[1, 144]], -15, 0)
+    iota(b12, [[1, 12]], 0, 0)
+    iota(p4, [[0, 1]], -31, 2)
+    iota(j6, [[32, 6]], -11, 2)
     iota(i12, [[0, 8], [1, 12]], 0, 0)
-    iota(j6, [[16, 6]], 0, 1)
-    kI, gI, hI = new("I", 1), new("I", 1), new("I", 1)
-    kc, gc, ec, oc, pg, pc = [new("F", 1) for i in range(6)]
-    vs(kI, pI, 15, None, OP.bitwise_and)
-    vs(gI, pI, 4, None, OP.arith_shift_right)
-    vs(hI, gI, 1, None, OP.bitwise_and)
-    vc(kc, kI); vc(gc, gI); vc(oc, hI); vc(pc, pI)
-    vs(ec, oc, -1.0, 1.0, OP.mult, OP.add)
-    vs(pg, gc, 16.0, None, OP.mult)
-    i15 = new("I", L)
-    diag, M0, RS = new("F", L), new("F", L), new("F", L)
-    vs(i15, iI, 15, None, OP.bitwise_and)
+    iota(iF, [[1, L]], 0, 0)
+    gc = col(col(p2, 1.0 / 32, MAGIC), 1.0, -MAGIC)
+    kc = col(gc, -16.0, pF)
+    ng, npg = col(gc, -1.0), col(gc, -16.0)
+    M0, diag = col(i15, 1.0, 0.0, AF.Sign), new("F", L)
     vs(diag, i15, kc, None, OP.is_equal)
-    vs(M0, i15, 0.0, None, OP.is_gt)
-    act(RS, M0, AF.Identity, 2.0e9, -1.0e9)
-    U, UW, wc = new("B", 144), new("B", 144), new("F", 1)
-    vs(U, xI, pg, None, OP.is_equal)
+    U, wc = same(xF, npg, "B"), new("F", 1)
     vc(wc, wI)
-    vs(UW, U, wc, None, OP.mult)
-    ygI, BO, sel8 = new("I", 128), new("H", 128), new("H", 128)
-    vs(ygI, yI, 4, None, OP.arith_shift_right)
-    vs(BO, ygI, gc, None, OP.is_equal)
-    vs(r(sel8, p1=8), r(ygI, p1=8), r(pc, p1=8), None, OP.is_equal)
-    ph16, th16, thc = new("H", L), new("H", 3), new("F", 3)
+    UW = tile(U, wc)
+    sel8, ph16, th16, thc = new("H", 128), new("H", L), new("H", 3), new("F", 3)
+    vs(r(sel8, p1=8), r(yg, p1=8), r(pF, p1=8), None, OP.is_equal)
     vs(r(ph16, p1=8), r(phI, p1=8), -2048.0, None, OP.add)
     vs(r(th16, p1=8), r(thI, p1=8), 0.0, None, OP.add)
     xq = place("xc", L)
@@ -213,102 +213,80 @@ def build(ne):
     pm, ps, phi = new("F", L), new("F", L), new("F", 12)
     vt(pm, xq, diag, OP.mult)
     vscan(ps, M0, pm, 0.0, OP.mult, OP.add)
-    vs(phi, r(ps, 15, L, 16), 2048.0, None, OP.add)
+    act(phi, r(ps, 15, L, 16), AF.Identity, 1.0, 2048.0)
     tp = r(place("u", 12), 0, 3)
     mm([(tp, r(sel8, p1=8), r(th16, p1=8), True, True)])
-    vc(thc, tp)
-    dumR, dumC, i16A, bl = new("F", 12), new("F", 12), new("F", 12), new("U", 12)
-    vs(i16A, bI, 16.0, kc, OP.mult, OP.add)
-    act(dumR, i16A, AF.Identity, 1.0, float(NR))
-    act(dumC, i16A, AF.Identity, 1.0, float(NC))
-    dumS, dumRC = new("F", 12), new("F", 24)
-    act(dumS, dumR, AF.Identity, 1.0, -1536.0)
+    act(thc, tp, AF.Copy)
+    for x in (0, 1):
+        vc(("cel_t", 1024 * x, 1024), ("cel_i", 1024 * x, 1024))
+    BO = same(yg, ng, "B")
+    lane, bl = col(b12, 16.0, kc), new("U", 12)
+    i16A, dumR, dumC, dumS = col(lane, 16.0), col(lane, 1.0, float(NR)), col(lane, 1.0, float(NC)), col(lane, 1.0, NR - 1536.0)
+    dumRC = new("F", 24)
     act(r(dumRC, 0, 12), dumR, AF.Copy)
     act(r(dumRC, 12, 24), dumC, AF.Copy)
-    act(i16A, i16A, AF.Identity, 16.0)
-    vc(bl, bI)
-    m3, m1, bo8 = new("B", 8), new("B", 8), new("B", 8)
-    vc(bo8, r(BO, 0, 128, 16))
-    act(m3, bo8, AF.Identity, -3.0)
-    act(m1, bo8, AF.Identity, -1.0)
-    one = new("B", 128)
-    vm(one, 1.0)
-    DW, MSK, list2 = new("B", 240), new("F", 96), new("U", 6)
-    vm(DW, 0.0)
-    vc(r(DW, 112, 128), r(diag, 0, 16))
-    mb1 = new("F", 96)
-    vs(mb1, i12, 8.0, 4.0, OP.is_ge, OP.mult)
-    vt(mb1, i12, mb1, OP.subtract)
-    vs(MSK, mb1, gc, None, OP.is_equal)
-    ja, jb, jf = new("I", 6), new("I", 6), new("F", 6)
-    vs(jf, j6, pg, None, OP.subtract)
-    vs(ja, jf, 1.0 / 12, 0.5 / 12 - 0.5, OP.mult, OP.add)
-    vs(jb, jf, 1.0 / 12, 4.5 / 12 - 0.5, OP.mult, OP.add)
-    vt(jf, ja, jb, OP.add)
-    vc(list2, jf)
-    pw, d16, scol, t1c, hf = new("F", 16), new("F", 16), new("F", 1), new("F", 1), new("F", 32)
-    vm(r(hf, 0, 16), 0.5); vm(r(hf, 16, 32), 0.0)
+    vc(bl, b12)
+    bo8 = new("B", 8)
+    act(bo8, r(BO, 0, 128, 16), AF.Copy)
+    m3, m1, one = tile(bo8, -3.0), tile(bo8, -1.0), tile(BO, 0.0, 1.0)
+    RS = col(M0, 2.0e9, -1.0e9)
+    DW, mb1, mb2, list2 = new("B", 240), new("F", 96), new("F", 96), new("U", 6)
+    act(r(DW, 0, 192), M0, AF.Identity, 0.0)
+    act(r(DW, 192, 240), r(M0, 0, 48), AF.Identity, 0.0)
+    act(r(DW, 112, 128), r(diag, 0, 16), AF.Copy)
+    vs(mb1, i12, 8.0, -4.0, OP.is_ge, OP.mult)
+    vt(mb2, mb1, i12, OP.add)
+    MSK = same(mb2, ng)
+    t1 = col(j6, 1.0, col(npg, 2.0))
+    y1, y2, js = col(col(t1, 1.0 / 24, MAGIC), 1.0, -MAGIC), col(col(col(t1, 1.0, 8.0), 1.0 / 24, MAGIC), 1.0, -MAGIC), new("F", 6)
+    vt(js, y1, y2, OP.add)
+    vc(list2, js)
+    oc = col(col(col(p4, 1.0 / 64, MAGIC), 1.0, -MAGIC), -2.0, gc)
+    ec = col(oc, -1.0, 1.0)
+    klt = col(col(kc, -1.0, 11.5, AF.Sign), 1.0, 0.0, AF.Relu)
+    k0, k10, k11, k12, k13 = [same(kc, -float(v)) for v in (0, 10, 11, 12, 13)]
+    hf, pw, pw2, d16, d17, sc0, sc2 = new("F", 48), new("F", 16), new("F", 16), new("F", 16), new("F", 16), new("F", 1), new("F", 1)
+    for x, v in ((0, 0.5), (16, 0.0), (32, 2.0)):
+        act(r(hf, x, x + 16), r(M0, 0, 16), AF.Identity, 0.0, v)
     vscan(pw, r(hf, 0, 16), r(hf, 16, 32), 2.0, OP.mult, OP.add)
+    vscan(pw2, r(hf, 32, 48), r(hf, 16, 32), 0.5, OP.mult, OP.add)
     vt(d16, pw, r(diag, 0, 16), OP.mult)
-    vred(scol, d16)
-    klt, k10, k11, k12, k13 = [new("F", 1) for i in range(5)]
-    vs(klt, kc, 12.0, None, OP.is_lt)
-    for kk, v in ((k10, 10.0), (k11, 11.0), (k12, 12.0), (k13, 13.0)):
-        vs(kk, kc, v, None, OP.is_equal)
-    vt(scol, scol, klt, OP.mult)
-    vs(t1c, klt, -0.5, None, OP.mult)
-    fb, fs, gb, gs, fbe, fse, fbo, fso, t2c = [new("F", 1) for i in range(9)]
-    vs(t2c, k10, 2.0, t1c, OP.mult, OP.add)
-    vt(fb, t2c, k12, OP.add)
-    vt(gb, t2c, k13, OP.add)
-    vs(fs, k13, -1.0 / 512, klt, OP.mult, OP.add)
-    vs(gs, k12, 1.0 / 512, klt, OP.mult, OP.add)
-    vt(fbe, fb, ec, OP.mult); vt(fse, fs, ec, OP.mult); vt(fbo, fb, oc, OP.mult); vt(fso, fs, oc, OP.mult)
-    I16, L16, laneC, t128, kv = new("H", 128), new("H", 128), new("H", L), new("F", 128), new("F", 1)
-    vs(I16, wyp, 0.0, None, OP.is_equal)
-    vs(kv, kc, 0.0, None, OP.is_gt)
-    vt(kv, kv, klt, OP.mult)
-    vs(kv, kv, -2.0, None, OP.mult)
-    vs(t128, wyp, -1.0, kv, OP.is_equal, OP.mult)
-    vt(L16, t128, I16, OP.add)
-    vt(t1c, k12, k13, OP.add)
-    vs(laneC, iI, t1c, None, OP.mult)
-    TL, TH, tl = new("B", 128), new("B", 128), new("F", 128)
-    vs(tl, wyp, 0.0, None, OP.is_gt)
-    vt(tl, tl, BO, OP.mult)
-    vt(TL, I16, tl, OP.subtract)
-    vs(t128, wyp, 0.0, None, OP.is_lt)
-    vt(t128, t128, BO, OP.mult)
-    vt(TH, I16, t128, OP.subtract)
-    nI, hI16, kI16, q25 = new("B", 128), new("B", 128), new("B", 128), new("B", L)
-    vs(nI, wyp, 0.0, -1.0, OP.is_equal, OP.mult)
-    act(hI16, nI, AF.Identity, -0.5)
-    act(kI16, nI, AF.Identity, 1024.0)
-    act(q25, M0, AF.Identity, 0.0, -0.25)
-    C2, pw2, bM, hf2 = new("H", L), new("F", 16), new("F", 1), new("F", 16)
-    vm(hf2, 2.0)
-    vscan(pw2, hf2, r(hf, 16, 32), 0.5, OP.mult, OP.add)
-    vt(d16, pw2, r(diag, 0, 16), OP.mult)
-    vred(t2c, d16)
-    vs(t2c, t2c, -0.5, 0.5, OP.mult, OP.add)
-    vt(t2c, t2c, klt, OP.mult)
-    vs(C2, M0, 0.0, t2c, OP.mult, OP.add)
-    vs(bM, k11, MAGIC, None, OP.add)
+    vt(d17, pw2, r(diag, 0, 16), OP.mult)
+    vred(sc0, d16)
+    vred(sc2, d17)
+    scol = col(sc0, klt)
+    fs, gs = col(k13, -1.0 / 512, klt), col(k12, 1.0 / 512, klt)
+    fse, fso = col(fs, ec), col(fs, oc)
+    kv = col(col(kc, 1.0, 0.0, AF.Sign), klt)
+    fb0 = col(k10, 2.0, col(klt, -0.5))
+    fb, gb = col(fb0, 1.0, k12), col(fb0, 1.0, k13)
+    fbe, fbo = col(fb, ec), col(fb, oc)
+    C2, c2c, bM = new("H", L), col(col(sc2, -0.5, 0.5), klt), col(k11, 1.0, MAGIC)
+    vs(C2, M0, 0.0, c2c, OP.mult, OP.add)
+    b11 = col(col(scol, 0.5, col(klt, -0.5)), 1.0, col(kv, 1025.0))
+    f11 = col(k11, -2050.0, col(k0, 1025.0, col(klt, 1024.5)))
+    fb2, gb2 = col(f11, 1.0, k12), col(f11, 1.0, k13)
+    fbe2, fbo2 = col(fb2, ec), col(fb2, oc)
+    Y, GT, EQ, NE = [[1, 128]], OP.is_gt, OP.is_equal, OP.not_equal
+    I16, LA, L16, nBO, TA, TL, TB, TH = [new("B", 128) for i in range(8)]
+    KV = tile(one, col(kv, -2.0))
+    act(nBO, BO, AF.Identity, -1.0)
+    sel(I16, one, Y, 0, -1, 0.0, EQ)
+    sel(LA, KV, Y, 1, -1, 0.0, EQ)
+    sel(L16, LA, Y, 0, -1, 1.0, NE)
+    sel(TA, nBO, Y, 0, -1, 0.0, GT)
+    sel(TL, TA, Y, 0, -1, 1.0, NE)
+    sel(TB, nBO, [[-1, 128]], 0, 1, 0.0, GT)
+    sel(TH, TB, Y, 0, -1, 1.0, NE)
+    nI, hI16, kI16 = [tile(I16, v) for v in (-1.0, 0.5, -1024.0)]
+    laneC, c64 = tile(iF, col(k12, 1.0, k13)), tile(M0, 0.0, 64.0)
     pas, acc, cand, winB, vfB = [new("B", 16) for i in range(5)]
-    P = [[new("H", 128), new("H", 128)], [new("H", 128), new("H", 128)]]
-    vs(P[0][0], wyp, 0.0, ec, OP.is_equal, OP.mult)
-    vs(P[1][1], wyp, 0.0, oc, OP.is_equal, OP.mult)
-    vs(P[0][1], wyp, 16.0, ec, OP.is_equal, OP.mult)
-    vs(P[1][0], wyp, -16.0, oc, OP.is_equal, OP.mult)
-    knear = new("F", 1)
-    vs(knear, kc, -1.0 / 16, 255.0 + 15.0 / 16, OP.mult, OP.add)
-    c128, c64 = new("B", L), new("B", L)
-    act(c128, M0, AF.Identity, 0.0, 128.0)
-    act(c64, M0, AF.Identity, 0.0, 64.0)
-    vm(("rec_t", NR, L), 64.0)
-    vm(("po_t", NR, L), 0.0)
-    for h in (0, 1):
-        vc(("cel_t", 1024 * h, 1024), ("cel_i", 1024 * h, 1024))
+    P = [[tile(I16, ec), new("B", 128)], [new("B", 128), tile(I16, oc)]]
+    sel(P[0][1], tile(one, ec), Y, -16, -1, 0.0, EQ)
+    sel(P[1][0], tile(one, oc), Y, 16, -1, 0.0, EQ)
+    knear = col(kc, -1.0 / 16, 255.0 + 15.0 / 16)
+    act(("rec_t", NR, L), M0, AF.Identity, 0.0, 64.0)
+    act(("po_t", NR, L), M0, AF.Identity, 0.0)
     poF = new("F", L)
     vc(poF, poI)
     dma(lambda g, T: g.sync.dma_start(out=T.pod[:], in_=ap(T, r(poF))), spans(r(poF)), [("pod", 0, 1)], 2.2)
@@ -334,16 +312,21 @@ def build(ne):
         return X
 
     def pairs(val, E, site):
-        X, Vi, Vh = expand(val), new("F", L), new("H", L)
+        X, Vh, b = expand(val), new("H", L), site != "v"
         xP, fp = place("x" + site, L), place("f" + site, L)
-        mm([(xP, BO, X, True, False), (xP, I16, C2, False, True)])
-        act(Vi, xP, AF.Identity, scol, bM)
-        vs(Vh, Vi, -MAGIC, None, OP.add)
+        if b:
+            mm([(xP, BO, X, True, True)])
+            vs(Vh, xP, scol, b11, OP.mult, OP.add)
+        else:
+            Vi = new("F", L)
+            mm([(xP, BO, X, True, False), (xP, I16, C2, False, True)])
+            act(Vi, xP, AF.Identity, scol, bM)
+            vs(Vh, Vi, -MAGIC, None, OP.add)
         mm([(fp, L16, Vh, True, False), (fp, I16, laneC, False, True)])
         G, Fe, Fo = new("B", L), new("B", L), new("B", L)
-        act(Fe, fp, AF.Identity, fse, fbe)
-        act(G, fp, AF.Identity, gs, gb)
-        act(Fo, fp, AF.Identity, fso, fbo)
+        act(Fe, fp, AF.Identity, fse, fbe2 if b else fbe)
+        act(G, fp, AF.Identity, gs, gb2 if b else gb)
+        act(Fo, fp, AF.Identity, fso, fbo2 if b else fbo)
         for a in range(4):
             bank, ms = ("e1", "e0")[a & 1], []
             for x, F in ((0, Fe), (1, Fo)):
@@ -463,13 +446,10 @@ def build(ne):
         act(sc32, ind(celn, c16), AF.Copy)
         act(skN, sc32, AF.Identity, 2.0 ** -16, knear)
         vs(s16c, sc16, -1536.0, None, OP.add)
-        cm, em = new("F", 12), new("F", 12)
-        vs(cm, c, -1024.0, None, OP.add)
         cur[0] = "E1"
-        E1 = pairs(cm, Es[0], "c")
+        E1 = pairs(c, Es[0], "c")
         cur[0] = "E2"
-        vs(em, e, -1024.0, None, OP.add)
-        E2 = pairs(em, Es[1], "e")
+        E2 = pairs(e, Es[1], "e")
         cur[0] = "n"
         nm = new("F", 12)
         act(nm, n, AF.Identity, 1.0, -1536.0)
@@ -502,15 +482,15 @@ def build(ne):
         vt(Dh, Dp, has, OP.mult)
         cur[0] = "newz"
         hP, tP, zP = place("hP", L), place("tP", L), place("zP", L)
-        hs, rz, zw, zm, zn = new("B", L), new("B", L), new("B", L), new("F", L), new("B", L)
+        hs, rz, zw, zm, zn = [new("B", L) for i in range(5)]
         mm([(hP, BO, q2, True, True)])
         act(hs, hP, AF.Sign, -1.0)
         act(rz, ind(recw, ny16), AF.Copy)
         mm([(tP, I16, rz, True, False), (tP, nI, z, False, True)])
         vt(zw, hs, tP, OP.mult)
-        mm([(zP, I16, z, True, False), (zP, hI16, zw, False, False), (zP, I16, q25, False, True)])
-        act(zm, zP, AF.Identity, 1.0, MAGIC)
-        act(zn, zm, AF.Identity, 1.0, -MAGIC)
+        mm([(zP, I16, z, True, False), (zP, hI16, zw, False, True)])
+        act(zm, zP, AF.Identity, 1.0, 159.75)
+        act(zn, zm, AF.Identity, 1.0, -160.0)
         send(zn, "zl%d" % (t + 1), "rz%d" % (t + 1))
         cur[0] = "far"
         vP, fd = best(K2, "far", ((0, L),))
@@ -535,8 +515,8 @@ def build(ne):
         ph2, phL, lP = new("F", 12), new("F", L), place("lP", L)
         act(ph2, phN, AF.Identity, 1.0, -2048.0)
         X = expand(ph2)
-        mm([(lP, BO, X, True, False), (lP, BO, c128, False, True)])
-        act(phL, lP, AF.Identity)
+        mm([(lP, BO, X, True, True)])
+        act(phL, lP, AF.Identity, 1.0, 2048.0)
         if last:
             send(phL, "pl%d" % VIS, "rp%d" % VIS)
         else:
@@ -607,14 +587,12 @@ def depend(ops):
         d = set()
         acc = [(s, False) for s in o["r"]] + [(s, True) for s in o["w"]]
         for (buf, lo, hi), wr in acc:
-            ps = buf in BANKS
             for (k, a, b, w) in hist.get(buf, []):
-                hit = (w or wr) and a < hi and lo < b
-                if (ops[k]["q"] != o["q"] or (o["q"] != "p" and hit)) if ps else hit:
+                if (w or wr) and a < hi and lo < b:
                     d.add(k)
         for (buf, lo, hi), wr in acc:
             hh = hist.setdefault(buf, [])
-            if wr and buf not in BANKS:
+            if wr:
                 hist[buf] = hh = [x for x in hh if not (lo <= x[1] and x[2] <= hi)]
             hh.append((o["i"], lo, hi, wr))
         d.discard(o["i"])
@@ -634,23 +612,31 @@ def schedule(ops, deps):
         pr[i] = ops[i]["cost"] + max([lat(i, j) + pr[j] for j in succ[i]] or [0.0])
     left = [len(d) for d in deps]
     ready = {i for i in range(n) if not left[i]}
-    rt, free, order, end = [0.0] * n, {}, [], [0.0] * n
+    banks = [sorted(set(s[0] for s in o["r"] + o["w"] if s[0] in BANKS)) for o in ops]
+    rt, free, order, end, used = [0.0] * n, {}, [], [0.0] * n, {b: {} for b in BANKS}
     while ready:
-        pick, cand = None, {}
+        pick, cand = None, {q: [] for q in ("v", "a", "p", "g", "s", "net")}
         for i in sorted(ready):
-            cand.setdefault(ops[i]["q"], []).append(i)
+            cand[ops[i]["q"]].append(i)
         for q, li in cand.items():
+            if not li:
+                continue
             f = free.get(q, 0.0) if q != "net" else 0.0
-            s0 = min(max(f, rt[i]) for i in li)
-            b = max((i for i in li if max(f, rt[i]) <= s0 + 0.04), key=lambda i: (pr[i] + BIAS.get(ops[i]["tag"], 0.0), -i))
-            s = max(f, rt[b])
-            if pick is None or s < pick[0]:
-                pick = (s, b, q)
+            at = {}
+            for i in li:
+                at[i] = max([f, rt[i]] + [end[k] + 0.12 for b in banks[i] for o, k in used[b].items() if o != q])
+            s0 = min(at.values())
+            b = max((i for i in li if at[i] <= s0 + 0.04), key=lambda i: (pr[i] + BIAS.get(ops[i]["tag"], 0.0), -i))
+            if pick is None or at[b] < pick[0]:
+                pick = (at[b], b, q)
         s, i, q = pick
         ready.discard(i)
         free[q] = s + (0.1 if q == "s" else ops[i]["cost"])
         end[i] = s + ops[i]["cost"]
         order.append(i)
+        for b in banks[i]:
+            deps[i] |= {k for o, k in used[b].items() if o != q}
+            used[b][q] = i
         for j in succ[i]:
             rt[j] = max(rt[j], end[i] + lat(i, j))
             left[j] -= 1

from concourse.mybir import AluOpType, AxisListType, ActivationFunctionType

OP = AluOpType
AF = ActivationFunctionType
L, NR, NC, VIS, STEP = 192, 3072, 2048, 3, 3
RW, CW = NR + L, NC + L
POOLS = {"F": 19000, "I": 2900, "U": 1600, "B": 33000, "H": 10200}
DTN = {"F": "float32", "I": "int32", "U": "uint16", "B": "bfloat16", "H": "float16"}
SCRATCH = {
    "rec_t": ("sbuf", [128, RW], "bfloat16"), "cel_t": ("sbuf", [128, CW], "float32"), "po_t": ("sbuf", [128, RW], "float32"),
    "cel_i": ("sbuf", [128, NC], "int32"), "pod": ("dram", [8, NR], "float32"),
    "zrep": ("sbuf", [128, 16 * L], "bfloat16"),
}
for _k in POOLS:
    SCRATCH["pool" + _k] = ("sbuf", [128, POOLS[_k]], DTN[_k])
for _t in range(1, VIS + 1):
    SCRATCH["zl%d" % _t] = ("sbuf", [128, L], "bfloat16")
    SCRATCH["pl%d" % _t] = ("sbuf", [128, 12 if _t < VIS else L], "float32")
BANKS = ["b0", "b1", "b2", "b3", "b4", "b5", "e0", "e1"]
for _b in BANKS:
    SCRATCH[_b] = ("psum", [128, 512], "float32")
SITE = {"dA": "b0", "kP": "b0", "hP": "b0", "tP": "b1", "zP": "b1", "vf": "b1", "ne": "b1", "de": "b2", "lP": "b2", "u": "b2", "s2": "b2",
        "near": "b3", "dB": "b3", "acc": "b3", "xv": "b3", "fv": "b3", "nv": "b3", "s1": "b4", "nc": "b4", "xe": "b4", "fe": "b4", "aP": "b4",
        "far": "b5", "xc": "b5", "fc": "b5", "win": "e0", "m1": "e0", "D1": "e0", "m2": "e1", "D2": "e1"}
SEMAPHORES = ["sv", "sa", "sp", "sg", "ls"] + ["d%d" % i for i in range(20)] + ["rz%d" % t for t in (1, 2, 3)] + ["rp%d" % t for t in (1, 2, 3)]
NS = 0.83 * 1.15e-3
MAGIC = 12582912.0
BIAS = {"ent11": 205, "early1": -530, "far1": 307, "ent12": 315, "far2": 112, "newz0": 492, "cg11": 736, "phL2": 73, "acc2": 31, "ent10": -55,
        "cg02": 227, "cg22": 638, "load": 630, "cg12": 434, "near2": -74, "eg12": 8, "ecell2": -5, "acc0": 73, "n0": -120, "ecell0": -376,
        "E21": 125, "n1": -151, "cg01": 238, "n2": -497, "lists2": 251, "ecell1": 3, "E20": -2, "zrep2": -222, "E31": 317, "early2": -60,
        "E30": 339, "cell2": 160, "cg10": 75, "eg01": 183, "eg02": 110, "newz2": -221, "eg21": 107, "ent20": 1, "phL0": -531, "slots0": 348,
        "newz1": 132, "zrep0": 67, "acc1": 106, "eg22": 159, "eg11": 20, "far0": 892, "cg20": -1, "cg21": 220, "phL1": -162, "ent21": -1,
        "slots2": 5, "near1": 242, "E32": -62, "E10": 112, "cg00": 605, "ent22": -73, "slots1": 218, "eg10": 5, "zrep1": -73, "cell0": 4,
        "lists0": -9, "lists1": -3, "near0": 2, "cell1": -1}
CACHE = {}


def build(ne):
    ops, top, ndma, cur, vis = [], {k: 0 for k in POOLS}, [0], ["load"], []

    def new(k, w):
        o = top[k]
        top[k] = o + (w + 15) // 16 * 16
        if top[k] > POOLS[k]:
            raise ValueError("pool %s is full" % k)
        return ("pool" + k, o, w)

    def r(t, c0=0, c1=None, st=1, p0=0, p1=128):
        return ("R", t[0], t[1] + c0, t[1] + (t[2] if c1 is None else c1), st, p0, p1)

    def ref(x):
        return x if isinstance(x, (int, float)) or x is None or x[0] in ("R", "X") else r(x)

    def ind(win, off):
        return ("X", ref(win), ref(off))

    ptop, sites = {b: 0 for b in BANKS}, {}

    def place(site, w):
        if site not in sites:
            b = SITE[site]
            sites[site] = (b, ptop[b], w)
            ptop[b] += w
            if ptop[b] > 512:
                raise ValueError("bank %s is full" % b)
        return sites[site]

    def spans(x):
        if x is None or isinstance(x, (int, float)):
            return []
        if x[0] == "X":
            return spans(x[1]) + spans(x[2])
        return [(x[1], x[2], x[3])]

    def ncol(x):
        return 16 * ncol(x[2]) if x[0] == "X" else (x[3] - x[2] + x[4] - 1) // x[4]

    def ap(T, x):
        if x is None or isinstance(x, (int, float)):
            return x
        if x[0] == "X":
            return ap(T, x[1]).indirect(ap(T, x[2]))
        t = T[x[1]]
        return t[x[5]:x[6], x[2]:x[3]] if x[4] == 1 else t[x[5]:x[6], x[2]:x[3]:x[4]]

    def two(x):
        return x[0] == "R" and x[1] in ("poolB", "poolH", "poolU", "zrep", "rec_t")

    def add(q, fn, reads, writes, cost, sem=None, val=1):
        ops.append({"q": q, "fn": fn, "r": reads, "w": writes, "cost": cost, "sem": sem, "val": val, "i": len(ops),
                    "tag": cur[0] + (str(vis[0]) if vis else "")})

    def vcost(o, ins, rate):
        n = ncol(o)
        if o[0] == "X":
            return 0.06 + n * 3.5 * NS
        if any(x[0] == "X" for x in ins):
            return 0.06 + n * 1.55 * NS
        return 0.02 + max(64, n * rate) * NS

    def vop(fn, outs, ins, cost):
        add("v", fn, [s for x in ins for s in spans(x)], [s for x in outs for s in spans(x)], cost)

    def vt(o, a, b, op):
        o, a, b = ref(o), ref(a), ref(b)
        both = a[0] == "R" and a[1] not in BANKS and b[1] not in BANKS
        vop(lambda g, T: g.vector.tensor_tensor(out=ap(T, o), in0=ap(T, a), in1=ap(T, b), op=op), [o], [a, b], vcost(o, [a, b], 2 if both else 1))

    def vs(o, a, s1, s2, op0, op1=None):
        o, a, s1, s2 = ref(o), ref(a), ref(s1), ref(s2)
        ex = {} if op1 is None else {"op1": op1}
        vop(lambda g, T: g.vector.tensor_scalar(out=ap(T, o), in0=ap(T, a), scalar1=ap(T, s1), scalar2=ap(T, s2), op0=op0, **ex),
            [o], [a, s1, s2], vcost(o, [a], 0.5 if two(o) and two(a) else 1))

    def vc(o, a):
        o, a = ref(o), ref(a)
        vop(lambda g, T: g.vector.tensor_copy(out=ap(T, o), in_=ap(T, a)), [o], [a], vcost(o, [a], 0.5 if two(o) and two(a) else 1))

    def vscan(o, d0, d1, init, o0, o1):
        o, d0, d1 = ref(o), ref(d0), ref(d1)
        vop(lambda g, T: g.vector.tensor_tensor_scan(out=ap(T, o), data0=ap(T, d0), data1=ap(T, d1), initial=init, op0=o0, op1=o1), [o], [d0, d1], vcost(o, [d0], 1))

    def vtr(o, a):
        o, a = ref(o), ref(a)
        vop(lambda g, T: g.vector.transpose(out=ap(T, o), in_=ap(T, a)), [o], [a], vcost(o, [a], 1))

    def vred(o, a):
        o, a = ref(o), ref(a)
        vop(lambda g, T: g.vector.tensor_reduce(out=ap(T, o), in_=ap(T, a), axis=AxisListType.X, op=OP.add), [o], [a], vcost(a, [a], 1))

    def act(o, a, f, scale=1.0, bias=0.0):
        o, a, scale, bias = ref(o), ref(a), ref(scale), ref(bias)
        x = a[0] == "X"
        add("a", lambda g, T: g.scalar.activation(out=ap(T, o), in_=ap(T, a), func=f, bias=ap(T, bias), scale=ap(T, scale)),
            [s for y in (a, scale, bias) for s in spans(y)], spans(o), (0.07 if x else 0.03) + max(64, ncol(o) * (1.55 if x else 1)) * NS)

    def mm(ms):
        ms = [(ref(o), ref(a), ref(b), s, e) for o, a, b, s, e in ms]

        def fn(g, T):
            k = None
            for o, a, b, s, e in ms:
                k = g.tensor.matmul(ap(T, o), ap(T, a), ap(T, b), s, e)
            return k
        rd = sorted(set(s for o, a, b, x, e in ms for y in (a, b) for s in spans(y)))
        add("p", fn, rd, sorted(set(s for m in ms for s in spans(m[0]))), sum(max(64, ncol(m[2])) for m in ms) * NS + 0.03)

    def iota(o, pat, base, cm):
        o = ref(o)
        add("g", lambda g, T: g.iota(ap(T, o), pat, base, cm, allow_small_or_imprecise_dtypes=True), [], spans(o), 0.13 + 2 * ncol(o) * NS)

    def sel(o, a, pat, base, cm, fill, cmp_):
        o, a = ref(o), ref(a)
        add("g", lambda g, T: g.affine_select(ap(T, o), ap(T, a), pat, cmp_, fill, base, cm), spans(a), spans(o), 0.17 + 2 * ncol(o) * NS)

    def dma(fn, reads, writes, cost, n=1):
        add("s", fn, reads, writes, cost, "d%d" % ndma[0], 16 * n)
        ndma[0] += 1

    z, wI, thI, phI, poI = new("B", L), new("I", 1), new("I", 3), new("I", L), new("I", L)

    def load(name, o, cost):
        o = ref(o)
        dma(lambda g, T: g.sync.dma_start(out=ap(T, o), in_=T[name][:]), [], spans(o), cost)
    load("phi", r(phI, p1=8), 2.2)
    load("pat", z, 2.2)
    load("wt", wI, 2.2)
    load("th", r(thI, p1=8), 2.2)
    for h in (0, 1):
        cs = ("cel_i", 1024 * h, 1024)
        dma(lambda g, T, h=h: g.sync.dma_start(out=T.cel_i[:, 1024 * h:1024 * h + 1024], in_=T.cel[:, 1024 * h:1024 * h + 1024]), [], spans(ref(cs)), 4.0 + 2 * h)
    dma(lambda g, T: g.sync.dma_start(out=T.rec_t[:, 0:NR], in_=T.rec[:]), [], [("rec_t", 0, NR)], 8.5)
    load("po", poI, 9.0)

    cur[0] = "const"

    def col(a, scale=1.0, bias=0.0, f=AF.Identity, k="F"):
        o = new(k, ref(a)[3] - ref(a)[2])
        act(o, a, f, scale, bias)
        return o

    def same(a, neg, k="F"):
        return col(col(a, 1.0, neg, AF.Abs), -1.0, 1.0, AF.Relu, k)

    def tile(a, scale, bias=0.0):
        return col(a, scale, bias, AF.Identity, "B")
    p2, pF, yg, i15, b12, j6, xF, iF = new("F", 1), new("F", 1), new("F", 128), new("F", L), new("F", 12), new("F", 6), new("F", 144), new("F", L)
    p4, i12 = new("F", 1), new("F", 96)
    iota(p2, [[0, 1]], -15, 2)
    iota(pF, [[0, 1]], 0, 1)
    iota(yg, [[1, 8], [0, 16]], 0, 0)
    iota(i15, [[0, 12], [1, 16]], 0, 0)
    iota(xF, [[1, 144]], -15, 0)
    iota(b12, [[1, 12]], 0, 0)
    iota(p4, [[0, 1]], -31, 2)
    iota(j6, [[32, 6]], -11, 2)
    iota(i12, [[0, 8], [1, 12]], 0, 0)
    iota(iF, [[1, L]], 0, 0)
    gc = col(col(p2, 1.0 / 32, MAGIC), 1.0, -MAGIC)
    kc = col(gc, -16.0, pF)
    ng, npg = col(gc, -1.0), col(gc, -16.0)
    M0, diag = col(i15, 1.0, 0.0, AF.Sign), new("F", L)
    vs(diag, i15, kc, None, OP.is_equal)
    U, wc = same(xF, npg, "B"), new("F", 1)
    vc(wc, wI)
    UW = tile(U, wc)
    sel8, ph16, th16, thc = new("H", 128), new("H", L), new("H", 3), new("F", 3)
    vs(r(sel8, p1=8), r(yg, p1=8), r(pF, p1=8), None, OP.is_equal)
    vs(r(ph16, p1=8), r(phI, p1=8), -2048.0, None, OP.add)
    vs(r(th16, p1=8), r(thI, p1=8), 0.0, None, OP.add)
    xq = place("xc", L)
    mm([(xq, r(sel8, p1=8), r(ph16, p1=8), True, True)])
    pm, ps, phi = new("F", L), new("F", L), new("F", 12)
    vt(pm, xq, diag, OP.mult)
    vscan(ps, M0, pm, 0.0, OP.mult, OP.add)
    act(phi, r(ps, 15, L, 16), AF.Identity, 1.0, 2048.0)
    tp = r(place("u", 12), 0, 3)
    mm([(tp, r(sel8, p1=8), r(th16, p1=8), True, True)])
    act(thc, tp, AF.Copy)
    for x in (0, 1):
        vc(("cel_t", 1024 * x, 1024), ("cel_i", 1024 * x, 1024))
    BO = same(yg, ng, "B")
    lane, bl = col(b12, 16.0, kc), new("U", 12)
    i16A, dumR, dumC, dumS = col(lane, 16.0), col(lane, 1.0, float(NR)), col(lane, 1.0, float(NC)), col(lane, 1.0, NR - 1536.0)
    dumRC = new("F", 24)
    act(r(dumRC, 0, 12), dumR, AF.Copy)
    act(r(dumRC, 12, 24), dumC, AF.Copy)
    vc(bl, b12)
    bo8 = new("B", 8)
    act(bo8, r(BO, 0, 128, 16), AF.Copy)
    m3, m1, one = tile(bo8, -3.0), tile(bo8, -1.0), tile(BO, 0.0, 1.0)
    RS = col(M0, 2.0e9, -1.0e9)
    DW, mb1, mb2, list2 = new("B", 240), new("F", 96), new("F", 96), new("U", 6)
    act(r(DW, 0, 192), M0, AF.Identity, 0.0)
    act(r(DW, 192, 240), r(M0, 0, 48), AF.Identity, 0.0)
    act(r(DW, 112, 128), r(diag, 0, 16), AF.Copy)
    vs(mb1, i12, 8.0, -4.0, OP.is_ge, OP.mult)
    vt(mb2, mb1, i12, OP.add)
    MSK = same(mb2, ng)
    t1 = col(j6, 1.0, col(npg, 2.0))
    y1, y2, js = col(col(t1, 1.0 / 24, MAGIC), 1.0, -MAGIC), col(col(col(t1, 1.0, 8.0), 1.0 / 24, MAGIC), 1.0, -MAGIC), new("F", 6)
    vt(js, y1, y2, OP.add)
    vc(list2, js)
    oc = col(col(col(p4, 1.0 / 64, MAGIC), 1.0, -MAGIC), -2.0, gc)
    ec = col(oc, -1.0, 1.0)
    klt = col(col(kc, -1.0, 11.5, AF.Sign), 1.0, 0.0, AF.Relu)
    k0, k10, k11, k12, k13 = [same(kc, -float(v)) for v in (0, 10, 11, 12, 13)]
    hf, pw, pw2, d16, d17, sc0, sc2 = new("F", 48), new("F", 16), new("F", 16), new("F", 16), new("F", 16), new("F", 1), new("F", 1)
    for x, v in ((0, 0.5), (16, 0.0), (32, 2.0)):
        act(r(hf, x, x + 16), r(M0, 0, 16), AF.Identity, 0.0, v)
    vscan(pw, r(hf, 0, 16), r(hf, 16, 32), 2.0, OP.mult, OP.add)
    vscan(pw2, r(hf, 32, 48), r(hf, 16, 32), 0.5, OP.mult, OP.add)
    vt(d16, pw, r(diag, 0, 16), OP.mult)
    vt(d17, pw2, r(diag, 0, 16), OP.mult)
    vred(sc0, d16)
    vred(sc2, d17)
    scol = col(sc0, klt)
    fs, gs = col(k13, -1.0 / 512, klt), col(k12, 1.0 / 512, klt)
    fse, fso = col(fs, ec), col(fs, oc)
    kv = col(col(kc, 1.0, 0.0, AF.Sign), klt)
    fb0 = col(k10, 2.0, col(klt, -0.5))
    fb, gb = col(fb0, 1.0, k12), col(fb0, 1.0, k13)
    fbe, fbo = col(fb, ec), col(fb, oc)
    C2, c2c, bM = new("H", L), col(col(sc2, -0.5, 0.5), klt), col(k11, 1.0, MAGIC)
    vs(C2, M0, 0.0, c2c, OP.mult, OP.add)
    b11 = col(col(scol, 0.5, col(klt, -0.5)), 1.0, col(kv, 1025.0))
    f11 = col(k11, -2050.0, col(k0, 1025.0, col(klt, 1024.5)))
    fb2, gb2 = col(f11, 1.0, k12), col(f11, 1.0, k13)
    fbe2, fbo2 = col(fb2, ec), col(fb2, oc)
    Y, GT, EQ, NE = [[1, 128]], OP.is_gt, OP.is_equal, OP.not_equal
    I16, LA, L16, nBO, TA, TL, TB, TH = [new("B", 128) for i in range(8)]
    KV = tile(one, col(kv, -2.0))
    act(nBO, BO, AF.Identity, -1.0)
    sel(I16, one, Y, 0, -1, 0.0, EQ)
    sel(LA, KV, Y, 1, -1, 0.0, EQ)
    sel(L16, LA, Y, 0, -1, 1.0, NE)
    sel(TA, nBO, Y, 0, -1, 0.0, GT)
    sel(TL, TA, Y, 0, -1, 1.0, NE)
    sel(TB, nBO, [[-1, 128]], 0, 1, 0.0, GT)
    sel(TH, TB, Y, 0, -1, 1.0, NE)
    nI, hI16, kI16 = [tile(I16, v) for v in (-1.0, 0.5, -1024.0)]
    laneC, c64 = tile(iF, col(k12, 1.0, k13)), tile(M0, 0.0, 64.0)
    pas, acc, cand, winB, vfB = [new("B", 16) for i in range(5)]
    P = [[tile(I16, ec), new("B", 128)], [new("B", 128), tile(I16, oc)]]
    sel(P[0][1], tile(one, ec), Y, -16, -1, 0.0, EQ)
    sel(P[1][0], tile(one, oc), Y, 16, -1, 0.0, EQ)
    knear = col(kc, -1.0 / 16, 255.0 + 15.0 / 16)
    act(("rec_t", NR, L), M0, AF.Identity, 0.0, 64.0)
    act(("po_t", NR, L), M0, AF.Identity, 0.0)
    poF = new("F", L)
    vc(poF, poI)
    dma(lambda g, T: g.sync.dma_start(out=T.pod[:], in_=ap(T, r(poF))), spans(r(poF)), [("pod", 0, 1)], 2.2)
    fan_id = ndma[0]

    def fan(g, T):
        k = None
        for i in range(16):
            k = g.sync.dma_start(out=T.po_t[i::16, 0:NR], in_=T.pod[:])
            if i < 15:
                k.then_inc(T.sem["d%d" % fan_id], 16)
        return k
    dma(fan, [("pod", 0, 1)], [("po_t", 0, NR)], 7.0, 16)
    h = new("F", 1)
    vc(h, r(thc, 0, 1))
    celw, celn, recw, recn, pow_ = ("cel_t", 0, CW), ("cel_t", 0, NC), ("rec_t", 0, RW), ("rec_t", 0, NR), ("po_t", 0, RW)
    Es = [new("B", 2048) for x in range(3)]
    dfad = [(new("B", 1024), new("B", 1024)) for x in range(6)]

    def expand(src):
        X = new("H", L)
        vt(X, ind(src, bl), diag, OP.mult)
        return X

    def pairs(val, E, site):
        X, Vh, b = expand(val), new("H", L), site != "v"
        xP, fp = place("x" + site, L), place("f" + site, L)
        if b:
            mm([(xP, BO, X, True, True)])
            vs(Vh, xP, scol, b11, OP.mult, OP.add)
        else:
            Vi = new("F", L)
            mm([(xP, BO, X, True, False), (xP, I16, C2, False, True)])
            act(Vi, xP, AF.Identity, scol, bM)
            vs(Vh, Vi, -MAGIC, None, OP.add)
        mm([(fp, L16, Vh, True, False), (fp, I16, laneC, False, True)])
        G, Fe, Fo = new("B", L), new("B", L), new("B", L)
        act(Fe, fp, AF.Identity, fse, fbe2 if b else fbe)
        act(G, fp, AF.Identity, gs, gb2 if b else gb)
        act(Fo, fp, AF.Identity, fso, fbo2 if b else fbo)
        for a in range(4):
            bank, ms = ("e1", "e0")[a & 1], []
            for x, F in ((0, Fe), (1, Fo)):
                pp = {"p0": 32 * a, "p1": 32 * a + 32}
                ms.append(((bank, 256 * x, L), r(F, 0, 128, **pp), r(G, **pp), True, True))
                ms.append(((bank, 256 * x + L, 64), r(F, 64, L, **pp), r(G, 128, L, **pp), True, True))
            mm(ms)
            act(r(E, 512 * a, 512 * a + 512), (bank, 0, 512), AF.Relu, 512.0, -1536.0)
        return E

    def lowest(vec, E, site, out):
        q, ms = place("n" + site, 16), []
        for g in range(8):
            h0, h1 = r(vec, 2 * g, 2 * g + 1), r(vec, 2 * g + 1, 2 * g + 2, p0=64)
            ms.append((r(q, 2 * g, 2 * g + 1), r(E, 256 * g, 256 * g + 128), h0, True, True))
            ms.append((r(q, 2 * g + 1, 2 * g + 2), r(E, 256 * g + 64, 256 * g + L), h0, True, False))
            ms.append((r(q, 2 * g + 1, 2 * g + 2), r(E, 256 * g + 128, 256 * g + 256, p0=64), h1, False, True))
        mm(ms)
        vt(out, vec, q, OP.is_gt)
        return out

    def score(terms, site, extra=None):
        for q, a, b in ((r(place(site, 16), 0, 16, 2), 0, 128), (r(place(site, 16), 1, 16, 2), 64, L)):
            ms = [(q, r(x, a, b), y) for x, y in terms]
            if extra:
                ms.append((q, extra[0], extra[1]))
            mm([m + (i == 0, i == len(ms) - 1) for i, m in enumerate(ms)])

    def to_a(vec, site):
        X = new("B", 96)
        vt(X, ind(vec, list2), MSK, OP.mult)
        q = place(site, 12)
        mm([(q, r(DW, 112 - 16 * g, 240 - 16 * g), r(X, 12 * g, 12 * g + 12), g == 0, g == 7) for g in range(8)])
        return q

    def best(key, site, parts):
        kt, ks, q = new("F", L), new("F", L), place(site, 24)
        ki, k2, kp = new("I", 12), new("I", 24), new("H", 24)
        for a, b in parts:
            vtr(r(kt, a, b), r(key, a, b))
            vscan(r(ks, a, b), r(RS, a, b), r(kt, a, b), -1.0e9, OP.min, OP.max)
        vs(ki, r(ks, 15, L, 16), 65536.0, None, OP.mult)
        vs(r(k2, 0, 12), ki, 4095, None, OP.bitwise_and)
        vs(r(k2, 12, 24), ki, 16, None, OP.arith_shift_right)
        vs(kp, k2, -1536.0, None, OP.add)
        mm([(r(q, ih, 24, 2), P[ih][x], r(kp, x, 24, 2), x == 0, x == 1) for ih in (0, 1) for x in (0, 1)])
        return r(q, 0, 12), r(q, 12, 24)

    def send(src, name, sem):
        src = ref(src)

        def fn(g, T, me, dst, topo):
            rid, pid, se = topo.addr(dst)
            return g.remote_dma(T[name][:], ap(T, src), T.sem[sem], T.sem.ls, pid, rid, topo.mask(me, dst))
        add("g", fn, spans(src), [(name + "_sent", 0, 1)], 1.0, "ls", ne)
        add("net", None, [(name + "_sent", 0, 1)], [(name, 0, SCRATCH[name][1][1])], 2.5, sem, ne)

    for t in range(VIS):
        last = t == VIS - 1
        vis[:] = [t]
        cur[0] = "cell"
        h5, hm, h511, hmat, hdead = new("F", 1), new("F", 1), new("F", 1), new("H", 8), new("H", 8)
        act(h5, h, AF.Identity, 5.0)
        act(hm, h, AF.Identity, -1.0, 512.0)
        act(h511, h, AF.Identity, 1.0, -511.0)
        vs(hmat, bo8, h511, None, OP.mult)
        vs(hdead, bo8, hm, None, OP.mult)
        cur[0] = "zrep"
        for k in range(16):
            act(r(("zrep", 0, 16 * L), k, 16 * L, 16), z, AF.Copy)
        cur[0] = "cell"
        uP = place("u", 12)
        mm([(uP, r(UW, 15 - k, 143 - k), r(z, k, L, 16), k == 0, k == 15) for k in range(16)])
        uI, u, ma, mb, mc, c, c1, e = [new("I", 12) for i in range(8)]
        c16, e16 = new("U", 12), new("U", 12)
        vc(uI, uP)
        vs(u, uI, 4095, None, OP.bitwise_and)
        vt(ma, phi, u, OP.mult)
        vs(mb, ma, 5, None, OP.arith_shift_right)
        p77 = phi
        if t:
            p77 = new("F", 12)
            act(p77, phi, AF.Identity, 1.0, 77.0 * t)
        vt(mc, mb, p77, OP.add)
        vs(c, mc, NC - 1, None, OP.bitwise_and)
        vc(c16, c)
        sc16, se16 = new("U", L), new("U", L)
        vc(sc16, ind(celn, c16))
        cur[0] = "ecell"
        me, mf, mg = [new("I", 12) for i in range(3)]
        vt(me, c, u, OP.mult)
        vs(mf, me, 5, None, OP.arith_shift_right)
        vs(c1, c, 1.0, None, OP.add)
        vt(mg, mf, c1, OP.add)
        vs(e, mg, NC - 1, None, OP.bitwise_and)
        vc(e16, e)
        vc(se16, ind(celn, e16))
        dc = lambda a, b: r(place("dA", 128), a, b) if b <= 128 else r(place("dB", 64), a - 128, b - 128)
        for s16, dst in ((sc16, dc), (se16, lambda a, b: r(place("de", L), a, b))):
            for ch in range(3):
                cur[0] = ("cg" if s16 is sc16 else "eg") + str(ch)
                df, ad = dfad[ch + (0 if s16 is sc16 else 3)]
                for x in (0, 1):
                    w = 1024 * ch + 512 * x
                    vt(r(df, 512 * x, 512 * x + 512), ind(recn, r(s16, 64 * ch + 32 * x, 64 * ch + 32 * x + 32)), ("zrep", w, 512), OP.subtract)
                    act(r(ad, 512 * x, 512 * x + 512), r(df, 512 * x, 512 * x + 512), AF.Abs)
                q = dst(64 * ch, 64 * ch + 64)
                mm([(q, r(U, 15 - k, 143 - k), r(ad, k, 1024, 16), k == 0, k == 15) for k in range(16)])
        cur[0] = "early"
        n15, n, pa, pb, P2 = new("I", 12), new("F", 12), new("F", 12), new("I", 12), new("I", 12)
        vs(n15, u, 15, None, OP.bitwise_and)
        vt(n, n15, i16A, OP.add)
        act(pa, phi, AF.Identity, 5.0)
        vt(pb, pa, u, OP.add)
        vs(P2, pb, 4095, None, OP.bitwise_and)
        skN, sc32, s16c = new("F", L), new("F", L), new("H", L)
        act(sc32, ind(celn, c16), AF.Copy)
        act(skN, sc32, AF.Identity, 2.0 ** -16, knear)
        vs(s16c, sc16, -1536.0, None, OP.add)
        cur[0] = "E1"
        E1 = pairs(c, Es[0], "c")
        cur[0] = "E2"
        E2 = pairs(e, Es[1], "e")
        cur[0] = "n"
        nm = new("F", 12)
        act(nm, n, AF.Identity, 1.0, -1536.0)
        Xn = expand(nm)
        cur[0] = "slots"
        q1, q2, K1, K2, dead = new("H", L), new("H", L), new("F", L), new("F", L), new("B", L)
        for a, b in ((0, 128), (128, L)):
            d = dc(a, b)
            vt(r(K1, a, b), r(skN, a, b), d, OP.subtract)
            vs(r(q1, a, b), d, 512.0, -511.0, OP.min, OP.add)
            vs(r(q2, a, b), r(q1, a, b), h511, h511, OP.min, OP.subtract)
            vs(r(dead, a, b), r(q1, a, b), 1.0, None, OP.is_ge)
        cur[0] = "far"
        kP = place("kP", L)
        mm([(kP, I16, q1, True, False), (kP, kI16, dead, False, True)])
        vt(K2, skN, kP, OP.add)
        cur[0] = "near"
        nyP, dd = best(K1, "near", ((0, 128), (128, L)))
        ny16, d5, has = new("U", 12), new("F", 12), new("F", 12)
        vs(ny16, nyP, 1536.0, None, OP.add)
        act(d5, dd, AF.Identity, -5.0, 1275.0 - 5 * 1536.0)
        vs(has, d5, h5, None, OP.is_lt)
        pog, pos, pd, Pa, P1, Dp, Dh = new("F", L), new("F", L), new("F", 12), new("I", 12), new("I", 12), new("F", 12), new("F", 12)
        vt(pog, ind(pow_, ny16), diag, OP.mult)
        vscan(pos, M0, pog, 0.0, OP.mult, OP.add)
        vt(pd, d5, phi, OP.add)
        vt(Pa, r(pos, 15, L, 16), pd, OP.add)
        vs(P1, Pa, 4095, None, OP.bitwise_and)
        vt(Dp, P1, P2, OP.subtract)
        vt(Dh, Dp, has, OP.mult)
        cur[0] = "newz"
        hP, tP, zP = place("hP", L), place("tP", L), place("zP", L)
        hs, rz, zw, zm, zn = [new("B", L) for i in range(5)]
        mm([(hP, BO, q2, True, True)])
        act(hs, hP, AF.Sign, -1.0)
        act(rz, ind(recw, ny16), AF.Copy)
        mm([(tP, I16, rz, True, False), (tP, nI, z, False, True)])
        vt(zw, hs, tP, OP.mult)
        mm([(zP, I16, z, True, False), (zP, hI16, zw, False, True)])
        act(zm, zP, AF.Identity, 1.0, 159.75)
        act(zn, zm, AF.Identity, 1.0, -160.0)
        send(zn, "zl%d" % (t + 1), "rz%d" % (t + 1))
        cur[0] = "far"
        vP, fd = best(K2, "far", ((0, L),))
        vm_, riv, vd, vdr = new("F", 12), new("F", 12), new("F", 12), new("F", 12)
        vs(riv, fd, 256.0 + 1536.0, h, OP.add, OP.is_ge)
        vt(vd, vP, dumS, OP.subtract)
        vt(vdr, vd, riv, OP.mult)
        vt(vm_, vdr, dumS, OP.add)
        cur[0] = "E3"
        E3 = pairs(vm_, Es[2], "v")
        cur[0] = "acc"
        score([(q1, m1), (q2, m3), (dead, hdead)], "s1", (one, hmat))
        vs(pas, place("s1", 16), 0.0, None, OP.is_ge)
        lowest(pas, E1, "c", acc)
        accA = to_a(acc, "acc")
        ft, phN = new("F", 12), new("F", 12)
        vt(ft, Dh, accA, OP.mult)
        vt(phN, ft, P2, OP.add)
        if not last:
            send(phN, "pl%d" % (t + 1), "rp%d" % (t + 1))
        cur[0] = "phL"
        ph2, phL, lP = new("F", 12), new("F", L), place("lP", L)
        act(ph2, phN, AF.Identity, 1.0, -2048.0)
        X = expand(ph2)
        mm([(lP, BO, X, True, True)])
        act(phL, lP, AF.Identity, 1.0, 2048.0)
        if last:
            send(phL, "pl%d" % VIS, "rp%d" % VIS)
        else:
            aP, aF, aI, aJ = place("aP", 16), new("F", 1), new("I", 1), new("I", 1)
            mm([(r(aP, 0, 16, 2), one, r(acc, 0, 16, 2), True, True), (r(aP, 1, 16, 2), r(one, p0=64), r(acc, 1, 16, 2, p0=64), True, True)])
            vred(aF, aP)
            vc(aI, aF)
            vs(aJ, aI, 31, None, OP.bitwise_and)
        cur[0] = "E3"
        vfA = to_a(lowest(acc, E3, "v", vfB), "vf")
        tv, ov, v16 = new("F", 12), new("F", 12), new("U", 12)
        vt(tv, vdr, vfA, OP.mult)
        vt(ov, tv, dumR, OP.add)
        vc(v16, ov)
        cur[0] = "lists"
        nd_, cd_, tn, on, u24 = new("F", 12), new("F", 12), new("F", 24), new("F", 24), new("U", 24)
        vt(nd_, n, dumR, OP.subtract)
        vt(cd_, c, dumC, OP.subtract)
        vt(r(tn, 0, 12), nd_, accA, OP.mult)
        vt(r(tn, 12, 24), cd_, accA, OP.mult)
        vt(on, tn, dumRC, OP.add)
        vc(u24, on)
        n16, cw = r(u24, 0, 12), r(u24, 12, 24)
        vc(ind(recw, v16), c64)
        vc(ind(recw, n16), zn)
        vc(ind(pow_, n16), phL)
        cur[0] = "ent1"
        M1, ch1, mP, DP = new("F", L), new("F", L), place("m1", L), place("D1", L)
        mm([(mP, TL, dead, True, True), (DP, BO, Xn, True, False), (DP, nI, s16c, False, True)])
        act(M1, mP, AF.Relu)
        vt(ch1, M1, DP, OP.mult)
        vt(ind(celw, cw), ch1, sc32, OP.add)
        cur[0] = "ent2"
        q1e, q2e, deade = new("H", L), new("H", L), new("B", L)
        vs(q1e, place("de", L), 512.0, -511.0, OP.min, OP.add)
        vs(q2e, q1e, h511, h511, OP.min, OP.subtract)
        vs(deade, q1e, 1.0, None, OP.is_ge)
        score([(q2e, m1)], "s2")
        vt(cand, acc, place("s2", 16), OP.is_gt)
        wA = to_a(lowest(cand, E2, "e", winB), "win")
        ed, et, eo, ew = new("F", 12), new("F", 12), new("F", 12), new("U", 12)
        vt(ed, e, dumC, OP.subtract)
        vt(et, ed, wA, OP.mult)
        vt(eo, et, dumC, OP.add)
        vc(ew, eo)
        M2, sE, s16e, ch2, mP, DP = new("F", L), new("F", L), new("H", L), new("F", L), place("m2", L), place("D2", L)
        act(sE, ind(celn, e16), AF.Copy)
        vs(s16e, sE, -1536.0, None, OP.add)
        mm([(mP, TH, deade, True, True), (DP, BO, Xn, True, False), (DP, nI, s16e, False, True)])
        act(M2, mP, AF.Relu)
        vt(ch2, M2, DP, OP.mult)
        vt(ind(celw, ew), ch2, sE, OP.add)
        if not last:
            h = new("F", 1)
            vt(h, aJ, r(thc, t + 1, t + 2), OP.add)
            z, phi = ("zl%d" % (t + 1), 0, L), ("pl%d" % (t + 1), 0, 12)
    dma(lambda g, T: g.sync.dma_start(out=T.ypat[:], in_=T["zl%d" % VIS][:]), [("zl%d" % VIS, 0, L)], [("ypat", 0, 1)], 2.2)
    dma(lambda g, T: g.sync.dma_start(out=T.yphi[:], in_=T["pl%d" % VIS][::16, :]), [("pl%d" % VIS, 0, L)], [("yphi", 0, 1)], 2.2)
    dma(lambda g, T: g.sync.dma_start(out=T.ypo[:], in_=T.po_t[::16, 0:NR]), [("po_t", 0, NR)], [("ypo", 0, 1)], 3.0)
    dma(lambda g, T: g.sync.dma_start(out=T.yrec[:], in_=T.rec_t[:, 0:NR]), [("rec_t", 0, NR)], [("yrec", 0, 1)], 5.0)
    dma(lambda g, T: g.sync.dma_start(out=T.ycel[:], in_=T.cel_t[:, 0:NC]), [("cel_t", 0, NC)], [("ycel", 0, 1)], 6.0)
    return ops


def depend(ops):
    hist, deps = {}, []
    for o in ops:
        d = set()
        acc = [(s, False) for s in o["r"]] + [(s, True) for s in o["w"]]
        for (buf, lo, hi), wr in acc:
            for (k, a, b, w) in hist.get(buf, []):
                if (w or wr) and a < hi and lo < b:
                    d.add(k)
        for (buf, lo, hi), wr in acc:
            hh = hist.setdefault(buf, [])
            if wr:
                hist[buf] = hh = [x for x in hh if not (lo <= x[1] and x[2] <= hi)]
            hh.append((o["i"], lo, hi, wr))
        d.discard(o["i"])
        deps.append(d)
    return deps


def schedule(ops, deps):
    n = len(ops)
    succ = [[] for i in range(n)]
    for i, d in enumerate(deps):
        for k in d:
            succ[k].append(i)
    lat = lambda k, i: 0.05 if ops[k]["q"] == ops[i]["q"] else (0.12 if ops[k]["q"] != "net" else 0.3)
    pr = [0.0] * n
    for i in range(n - 1, -1, -1):
        pr[i] = ops[i]["cost"] + max([lat(i, j) + pr[j] for j in succ[i]] or [0.0])
    left = [len(d) for d in deps]
    ready = {i for i in range(n) if not left[i]}
    banks = [sorted(set(s[0] for s in o["r"] + o["w"] if s[0] in BANKS)) for o in ops]
    rt, free, order, end, used = [0.0] * n, {}, [], [0.0] * n, {b: {} for b in BANKS}
    while ready:
        pick, cand = None, {q: [] for q in ("v", "a", "p", "g", "s", "net")}
        for i in sorted(ready):
            cand[ops[i]["q"]].append(i)
        for q, li in cand.items():
            if not li:
                continue
            f = free.get(q, 0.0) if q != "net" else 0.0
            at = {}
            for i in li:
                at[i] = max([f, rt[i]] + [end[k] + 0.12 for b in banks[i] for o, k in used[b].items() if o != q])
            s0 = min(at.values())
            b = max((i for i in li if at[i] <= s0 + 0.04), key=lambda i: (pr[i] + BIAS.get(ops[i]["tag"], 0.0), -i))
            if pick is None or at[b] < pick[0]:
                pick = (at[b], b, q)
        s, i, q = pick
        ready.discard(i)
        free[q] = s + (0.1 if q == "s" else ops[i]["cost"])
        end[i] = s + ops[i]["cost"]
        order.append(i)
        for b in banks[i]:
            deps[i] |= {k for o, k in used[b].items() if o != q}
            used[b][q] = i
        for j in succ[i]:
            rt[j] = max(rt[j], end[i] + lat(i, j))
            left[j] -= 1
            if not left[j]:
                ready.add(j)
    return order, max(end)


QSEM = {"v": "sv", "a": "sa", "p": "sp"}


def plan(ne):
    if "plan" not in CACHE:
        ops = build(ne)
        deps = depend(ops)
        order, span = schedule(ops, deps)
        CACHE["plan"] = (ops, deps, order, span)
    return CACHE["plan"]


def rank_program(g, core, T, topo):
    rank = T.rank_of(core)
    if rank is None:
        return
    me, dst = T.cores[rank], T.cores[(rank + STEP) % len(T.cores)]
    ops, deps, order, span = plan(len(topo.engines(me, dst)))
    eng = {"v": g.vector, "a": g.scalar, "p": g.tensor, "g": g, "s": g.sync}
    at, count, seen = {}, {}, {}
    for i in order:
        o = ops[i]
        q = o["q"]
        sem = o["sem"] or QSEM.get(q, "sg")
        count[sem] = count.get(sem, 0) + o["val"]
        at[i] = (sem, count[sem])
        if q == "net":
            continue
        need = {}
        for k in deps[i]:
            s, v = at[k]
            if s == "ls" or (q == "p" and ops[k]["q"] == "p"):
                continue
            need[s] = max(need.get(s, 0), v)
        for s in sorted(need):
            if seen.get((q, s), 0) < need[s]:
                eng[q].wait_ge(T.sem[s], need[s])
                seen[(q, s)] = need[s]
        if o["sem"] == "ls":
            o["fn"](g, T, me, dst, topo)
        else:
            o["fn"](g, T).then_inc(T.sem[sem], 1 if o["sem"] is None else 16)
    for s in sorted(count):
        g.sync.wait_ge(T.sem[s], count[s])
